import numpy as np
import ml_dtypes


def mxq(x, axis, fmt="e4m3"):
    dtype, down = {"e4m3": (ml_dtypes.float8_e4m3fn, 7), "e5m2": (ml_dtypes.float8_e5m2, 14)}[fmt]
    v = np.moveaxis(np.asarray(x, np.float32).astype(ml_dtypes.bfloat16).astype(np.float64), axis, -1)
    blocks = v.reshape(v.shape[:-1] + (-1, 32))
    amax = np.abs(blocks).max(-1, keepdims=True)
    byte = np.maximum(np.where(amax > 0, np.frexp(amax)[1] - 1 + 127, 0) - down, 1)
    scale = np.exp2(byte - 127.0)
    codes = (blocks / scale).astype(np.float32).astype(dtype).astype(np.float64)
    return np.moveaxis((codes * scale).reshape(v.shape), -1, axis)


WIDE = False


def mx_kscale(k):
    if not WIDE:
        return np.ones(k)
    levels = np.array([10, -10, 5, -5, 0])
    if k % 512:
        return np.exp2(np.random.permutation(np.resize(levels, k // 32))).repeat(32)
    a = np.empty((k // 512, 16))
    for p in range(k // 512):
        a[p, :8] = np.random.permutation(np.resize(levels, 8))
        for g in range(8):
            far = levels[np.abs(levels - a[p, g]) >= 10]
            a[p, g + 8] = far[np.random.randint(len(far))]
    return np.exp2(a.ravel()).repeat(32)


def f64(x):
    return np.asarray(x).astype(np.float64)


def striped(idx):
    return np.tile(idx.reshape(-1, 16).T, (8, 1)).astype(np.uint16)


def unstriped(offs):
    return offs[:16].T.reshape(-1).astype(np.int64)


def striped8(idx):
    return np.concatenate([x.reshape(-1, 16).T for x in idx]).astype(np.uint16)


def runs(offs, k):
    lists = np.stack([offs[16 * r : 16 * r + 16].T.reshape(-1) for r in range(8)]).astype(np.int64)
    return lists[np.arange(k) % 512 // 64]


def pack_weight(w):
    k, n = w.shape
    w = f64(np.asarray(w, np.float32).astype(ml_dtypes.bfloat16)).reshape(k // 32, 32, n)
    amax = np.abs(w).max(1)
    byte = np.clip(np.where(amax > 0, np.frexp(amax)[1] - 1 + 127 - 7, 1), 1, 254)
    scaled = (w * np.exp2(127.0 - byte)[:, None, :]).reshape(k, n).astype(np.float32)
    words = np.ascontiguousarray(scaled.reshape(k // 512, 128, 4, n).transpose(0, 1, 3, 2)).astype(ml_dtypes.float8_e4m3fn).view(np.uint8)
    return words, np.ascontiguousarray(byte.astype(np.uint8).reshape(k // 512, 16, n))


def unpack_weight(words, scales):
    g, p, n, _ = words.shape
    vals = np.ascontiguousarray(words).view(ml_dtypes.float8_e4m3fn).astype(np.float64) * np.repeat(np.exp2(scales.astype(np.float64) - 127.0), 8, axis=1)[..., None]
    return vals.transpose(0, 1, 3, 2).reshape(g * 512, n)


def sigmoid(v):
    return 1.0 / (1.0 + np.exp(-np.maximum(v, -700.0)))

def planes(y):
    n, m = y.shape
    v = y.astype(np.float32).astype(ml_dtypes.bfloat16).astype(np.float64).reshape(n // 32, 32, m)
    top = np.abs(v).max(1)
    byte = np.clip(np.where(top > 0, np.frexp(top)[1] - 1 + 127 - 7, 1), 1, 254)
    codes = (v * np.exp2(127.0 - byte)[:, None, :]).reshape(n, m).astype(np.float32).astype(ml_dtypes.float8_e4m3fn).view(np.uint8)
    words = codes.reshape(n // 512, 128, 4, m).transpose(0, 1, 3, 2)
    return np.ascontiguousarray(words), np.ascontiguousarray(byte.astype(np.uint8).reshape(n // 512, 16, m))


K, T, S, N, H = 512, 2048, 512, 512, 512


def setup_inputs():
    n = np.random.standard_normal
    s = mx_kscale(K)[:, None]
    u = mx_kscale(S)
    packed_xT = pack_weight(n((K, T)) * s)
    return {
        "x_words": packed_xT[0],
        "x_scales": packed_xT[1],
        "wa": (n((K, H)) / np.sqrt(K) / s).astype(np.float32),
        "wb": (n((K, N)) / np.sqrt(K) / s).astype(np.float32),
        "gt": (np.random.uniform(0.5, 1.5, (S, 1)) * u[:, None]).astype(np.float32),
        "gi": (np.random.uniform(0.5, 1.5, (S, 1)) / u[:, None]).astype(np.float32),
        "offs": striped(np.random.permutation(T)[:S]),
        "two": striped(np.random.permutation(T)[:S]),
        "n1": striped8(np.stack([np.random.permutation(H) for _ in range(8)])),
        "n2": striped8(np.stack([np.random.permutation(H) for _ in range(8)])),
        "n3": striped8(np.stack([np.random.permutation(H) for _ in range(8)])),
        "n4": striped8(np.stack([np.random.permutation(N) for _ in range(8)])),
        "n5": striped8(np.stack([np.random.permutation(N) for _ in range(8)])),
    }


def reference(x_words, x_scales, wa, wb, gt, gi, offs, two, n1, n2, n3, n4, n5):
    xq = unpack_weight(x_words, x_scales)[:, unstriped(offs)]
    a = xq.T @ mxq(f64(wa), 0, "e4m3")
    b1 = a[np.arange(S)[:, None], runs(n1, S)]
    b2 = a[np.arange(S)[:, None], runs(n2, S)]
    b3 = a[np.arange(S)[:, None], runs(n3, S)]
    z = f64(gt) * (np.maximum(np.maximum(b1, b2), b3) - (0.5 * (np.maximum(np.minimum(b1, b2), np.minimum(np.maximum(b1, b2), b3)))))
    x_two = unpack_weight(x_words, x_scales)[:, unstriped(two)]
    b = x_two.T @ mxq(f64(wb), 0, "e4m3")
    z2 = f64(gi) * b
    cv = 0.0625 * ((mxq(z, 0, "e4m3").T @ mxq(z2, 0, "e4m3")))
    sm = np.maximum(cv, cv[np.arange(H)[:, None], runs(n5, H)])
    ds = np.zeros((H, N))
    ds[np.arange(H)[:, None], runs(n4, H)] = sm
    out_0 = ds * sigmoid(cv)
    return (out_0,) + planes(out_0)

@@ -1,0 +1,362 @@
+from contextlib import ExitStack
+
+import concourse.mybir as mybir
+from concourse.masks import make_identity
+
+K, T, S, H, N = 512, 2048, 512, 512, 512
+FLOPS = 3 * 2 * 512 * 512 * 512
+
+F32 = mybir.dt.float32
+BF16 = mybir.dt.bfloat16
+I32 = mybir.dt.int32
+U32 = mybir.dt.uint32
+U16 = mybir.dt.uint16
+U8 = mybir.dt.uint8
+FP8X4 = mybir.dt.float8_e4m3fn_x4
+ALU = mybir.AluOpType
+ACT = mybir.ActivationFunctionType
+
+P = 128
+PACK = 4
+W = 512
+WIN = 1024
+NPE = 3
+
+
+def tile_picked_momtop2sendg_none_po_kernel(
+    tc, x_words, x_scales, wa, wb, gt, gi, offs, two, n1, n2, n3, n4, n5, out_0, out_1, out_2
+):
+    nc = tc.nc
+    with ExitStack() as ctx:
+        lists = ctx.enter_context(tc.tile_pool(name="lists", bufs=1))
+        keep = ctx.enter_context(tc.tile_pool(name="keep", bufs=1))
+        ring = ctx.enter_context(tc.tile_pool(name="ring", bufs=2))
+        psum = ctx.enter_context(tc.psum_pool(name="psum", bufs=2))
+
+        def load_list(src, name):
+            tile = lists.tile([P, W // 16], U16, name=name)
+            nc.sync.dma_start(tile[:], src)
+            return tile
+
+        xs = keep.tile([P, T], U8, name="xs")
+        nc.gpsimd.memset(xs[:].bitcast(I32), 0)
+        grow = keep.tile([P, P], F32, name="grow")
+        nc.gpsimd.memset(grow[:], 0.0)
+        irow = keep.tile([P, P], F32, name="irow")
+        nc.gpsimd.memset(irow[:], 0.0)
+
+        def load_gate(rows, g):
+            nc.sync.dma_start(
+                rows[0:4, :].rearrange("t (b r) -> t b r", r=8),
+                g.rearrange("(b t r) o -> t b (r o)", t=PACK, r=8),
+            )
+
+        def load_weight(w, name, c0, c1):
+            raw = keep.tile([P, PACK, c1 - c0], F32, name=name)
+            nc.sync.dma_start(raw[:], w.rearrange("(p j) c -> p j c", j=PACK)[:, :, c0:c1])
+            return raw
+
+        offs_t = load_list(offs, "offs_t")
+        wa_raw = [load_weight(wa, "wa_raw0", 0, 256)]
+        for q in range(4):
+            nc.sync.dma_start(xs[32 * q : 32 * q + 4, :].bitcast(I32), x_scales[0, 4 * q : 4 * q + 4, :].bitcast(I32))
+        two_t = load_list(two, "two_t")
+        load_gate(grow, gt)
+        wa_raw.append(load_weight(wa, "wa_raw1", 256, 512))
+        xw = keep.tile([P, T], I32, name="xw")
+        nc.sync.dma_start(xw[:], x_words[0].rearrange("p n t -> p (n t)").bitcast(I32))
+        n1_t = load_list(n1, "n1_t")
+        n2_t = load_list(n2, "n2_t")
+        n3_t = load_list(n3, "n3_t")
+        wb_raw = load_weight(wb, "wb_raw", 0, W)
+        load_gate(irow, gi)
+        n5_t = load_list(n5, "n5_t")
+        n4_t = load_list(n4, "n4_t")
+
+        ident = keep.tile([P, P], F32, name="ident")
+        make_identity(nc, ident[:])
+        warm = keep.tile([P, 1], F32, name="warm")
+        nc.scalar.activation(warm[:], ident[:, 0:1], ACT.Sigmoid)
+
+        wins = []
+        for t in range(PACK):
+            win = keep.tile([P, WIN], F32, name=f"win{t}")
+            nc.gpsimd.memset(win[:, W:], 0.0)
+            wins.append(win)
+
+        def pick_scales(lst, name):
+            plain = keep.tile([P, W], U8, name=f"{name}_plain", align_bytes=64)
+            nc.vector.tensor_copy(plain[:], xs[:].indirect(lst[:]))
+            return plain
+
+        def deal_scales(plain, name):
+            dealt = keep.tile([P, W], U8, name=f"{name}_dealt", align_bytes=64)
+            nc.vector.tensor_copy(
+                dealt[:].bitcast(I32).rearrange("p (t b r) -> p b t r", t=PACK, r=2),
+                plain[:].bitcast(I32).rearrange("p (b t r) -> p b t r", t=PACK, r=2),
+            )
+            return dealt
+
+        def pick_words(lst, name):
+            words = keep.tile([P, W], I32, name=f"{name}_words", align_bytes=64)
+            nc.vector.tensor_copy(
+                words[:].bitcast(U32).rearrange("p (t b r) -> p b t r", t=PACK, r=8),
+                xw[:].bitcast(U32).indirect(lst[:]),
+            )
+            return words
+
+        def interleave(engine_copy, dst, src, c0, c1):
+            engine_copy(
+                dst[:, c0:c1, :].rearrange("p (c i) t -> p c t i", i=4),
+                src.rearrange("p t (c i) -> p c t i", i=4),
+            )
+
+        def mx_tiles(name):
+            grouped = keep.tile([P, W, PACK], BF16, name=f"{name}_bf", align_bytes=64)
+            codes = keep.tile([P, W], I32, name=f"{name}_codes", align_bytes=64)
+            scales = keep.tile([P, W], U8, name=f"{name}_scales", align_bytes=64)
+            return grouped, codes, scales
+
+        def quantise(mx, c0, c1):
+            grouped, codes, scales = mx
+            nc.vector.quantize_mx(
+                out=codes[:, c0:c1].bitcast(FP8X4),
+                scales=scales[:, c0:c1],
+                in_=grouped[:, c0:c1, :].rearrange("p c t -> p (c t)"),
+            )
+
+        def product(acc, words, scales, t, mx):
+            cols = slice(P * t, P * (t + 1))
+            nc.tensor.matmul_mx(
+                out=acc[:],
+                lhsT=words[:, cols].bitcast(FP8X4),
+                lhsT_scale=scales[:, cols],
+                rhs=mx[1][:].bitcast(FP8X4),
+                rhs_scale=mx[2][:],
+                start=True,
+                stop=True,
+            )
+
+        wa_mx = mx_tiles("wa")
+        wb_mx = mx_tiles("wb")
+        z_mx = mx_tiles("z")
+        z2_mx = mx_tiles("z2")
+        y_mx = mx_tiles("y")
+
+        sa_plain = pick_scales(offs_t, "sa")
+        sb_plain = pick_scales(two_t, "sb")
+        sa = deal_scales(sa_plain, "sa")
+        sb = deal_scales(sb_plain, "sb")
+        for h in range(2):
+            interleave(nc.scalar.copy, wa_mx[0], wa_raw[h][:], 256 * h, 256 * (h + 1))
+            quantise(wa_mx, 256 * h, 256 * (h + 1))
+        gps = psum.tile([P, W], F32, name="u_ps")
+        nc.tensor.transpose(gps[:, 0:P], grow[:], ident[:])
+        half_abs = keep.tile([P, PACK], F32, name="half_abs")
+        sign = keep.tile([P, PACK], F32, name="sign")
+        gis = keep.tile([P, PACK], F32, name="gis")
+        nc.scalar.activation(half_abs[:], gps[:, 0:4], ACT.Abs, scale=0.5)
+        nc.scalar.activation(sign[:], gps[:, 0:4], ACT.Sign)
+
+        xa = pick_words(offs_t, "xa")
+        for t in range(PACK):
+            acc = psum.tile([P, W], F32, name="a_ps")
+            product(acc, xa, sa, t, wa_mx)
+            nc.scalar.activation(wins[t][:, :W], acc[:], ACT.Copy, scale=half_abs[:, t : t + 1])
+        xb = pick_words(two_t, "xb")
+
+        zp = keep.tile([P, PACK, W], BF16, name="zp")
+        z2p = keep.tile([P, PACK, W], BF16, name="z2p")
+        st = {}
+
+        def new(name, t):
+            st[name, t] = ring.tile([P, W], F32, name=name)
+            return st[name, t]
+
+        def sl(part):
+            return slice(part[0], part[1]), slice(part[0] // 16, part[1] // 16)
+
+        whole = (0, W)
+
+        def step_a(t):
+            nc.vector.tensor_copy(new("b1", t)[:], wins[t][:].indirect(n1_t[:]))
+
+        def step_b(t):
+            nc.vector.tensor_tensor(new("x", t)[:], wins[t][:].indirect(n2_t[:]), st["b1", t][:], ALU.subtract)
+            nc.scalar.activation(new("ax", t)[:], st["x", t][:], ACT.Abs)
+
+        def step_c(t):
+            nc.vector.scalar_tensor_tensor(new("mx", t)[:], st["x", t][:], 0.0, st["b1", t][:], ALU.max, ALU.add)
+
+        def step_d(t, part):
+            c, o = sl(part)
+            if part[0] == 0:
+                new("e", t)
+                new("r", t)
+            nc.vector.tensor_tensor(st["e", t][:, c], wins[t][:].indirect(n3_t[:, o]), st["mx", t][:, c], ALU.subtract)
+            nc.scalar.activation(st["r", t][:, c], st["e", t][:, c], ACT.Relu, scale=3.0)
+
+        def step_e(t, part):
+            c, o = sl(part)
+            if part[0] == 0:
+                new("k", t)
+            nc.vector.scalar_tensor_tensor(st["k", t][:, c], st["e", t][:, c], -1.0, st["ax", t][:, c], ALU.mult, ALU.min)
+
+        def step_f(t, part):
+            c, o = sl(part)
+            if part[0] == 0:
+                new("q", t)
+            nc.vector.tensor_tensor(st["q", t][:, c], st["k", t][:, c], st["mx", t][:, c], ALU.add)
+
+        def step_g(t, part):
+            c, o = sl(part)
+            nc.vector.tensor_tensor(zp[:, t, c], st["q", t][:, c], st["r", t][:, c], ALU.add)
+
+        def sum_on_pe(t):
+            ups = psum.tile([P, W], F32, name="u_ps")
+            terms = [st["mx", t], st["r", t], st["k", t]]
+            for q in range(4):
+                c = slice(P * q, P * (q + 1))
+                for i, term in enumerate(terms):
+                    nc.tensor.matmul(ups[:, c], term[:, c], ident[:], start=(i == 0), stop=(i == 2), is_transpose=True)
+            ut = new("ut", t)
+            nc.scalar.copy(ut[:], ups[:])
+            zps = psum.tile([P, W], F32, name="z_ps")
+            for q in range(4):
+                c = slice(P * q, P * (q + 1))
+                nc.tensor.transpose(zps[:, c], ut[:, c], ident[:])
+            nc.scalar.copy(zp[:, t, :], zps[:])
+
+        def finish(t):
+            step_e(t, whole)
+            if t < NPE:
+                sum_on_pe(t)
+
+        def finish2(t):
+            if t >= NPE:
+                step_f(t, whole)
+
+        def finish3(t):
+            if t >= NPE:
+                step_g(t, whole)
+
+        def b_weights():
+            for h in range(2):
+                interleave(nc.scalar.copy, wb_mx[0], wb_raw[:, :, 256 * h : 256 * (h + 1)], 256 * h, 256 * (h + 1))
+            ips = psum.tile([P, W], F32, name="z_ps")
+            nc.tensor.transpose(ips[:, 0:P], irow[:], ident[:])
+            nc.vector.tensor_tensor(gis[:], ips[:, 0:4], sign[:], ALU.mult)
+
+        def b_product():
+            quantise(wb_mx, 0, W)
+            for t in range(PACK):
+                acc = psum.tile([P, W], F32, name="b_ps")
+                product(acc, xb, sb, t, wb_mx)
+                nc.scalar.activation(z2p[:, t, :], acc[:], ACT.Copy, scale=gis[:, t : t + 1])
+
+        def b_group(h):
+            interleave(nc.scalar.copy, z2_mx[0], z2p[:, :, 256 * h : 256 * (h + 1)], 256 * h, 256 * (h + 1))
+
+        step_a(0)
+        step_a(1)
+        step_b(0)
+        step_b(1)
+        b_weights()
+        step_c(0)
+        step_a(2)
+        step_d(0, whole)
+        step_c(1)
+        finish(0)
+        step_d(1, whole)
+        finish2(0)
+        b_product()
+        step_b(2)
+        finish3(0)
+        finish(1)
+        step_c(2)
+        finish2(1)
+        step_a(3)
+        finish3(1)
+        b_group(0)
+        step_d(2, whole)
+        step_b(3)
+        finish(2)
+        b_group(1)
+        step_c(3)
+        finish2(2)
+        halves = [(0, 256), (256, 512)]
+        step_d(3, halves[0])
+        finish3(2)
+        step_d(3, halves[1])
+        quantise(z2_mx, 0, W)
+        for step in (step_e, step_f, step_g):
+            for part in halves:
+                step(3, part)
+
+        def z_group(engine_copy, u):
+            engine_copy(
+                z_mx[0][:, P * u : P * (u + 1), :],
+                zp[:].rearrange("p t (m u) -> p u m t", u=4)[:, u],
+            )
+
+        z_group(nc.vector.tensor_copy, 0)
+        z_group(nc.scalar.copy, 1)
+        quantise(z_mx, 0, 128)
+        z_group(nc.vector.tensor_copy, 2)
+        quantise(z_mx, 128, 256)
+        z_group(nc.vector.tensor_copy, 3)
+        quantise(z_mx, 256, 512)
+
+        out_rows = out_0.rearrange("(p t) c -> p t c", t=PACK)
+        res = keep.tile([P, PACK, W], F32, name="res")
+        cv, sig, dif, rel, dss = {}, {}, {}, {}, {}
+
+        def moments(t):
+            acc = psum.tile([P, W], F32, name="a_ps" if t % 2 == 0 else "b_ps")
+            product(acc, z_mx[1], z_mx[2], t, z2_mx)
+            cv[t] = keep.tile([P, W], F32, name=f"cv{t}")
+            sig[t] = keep.tile([P, W], F32, name=f"sig{t}")
+            nc.scalar.activation(wins[t][:, :W], acc[:], ACT.Copy, scale=0.0625)
+            nc.scalar.activation(cv[t][:], acc[:], ACT.Copy, scale=0.0625)
+
+        def fetch(t):
+            dif[t] = keep.tile([P, W], F32, name=f"dif{t}")
+            rel[t] = keep.tile([P, W], F32, name=f"rel{t}")
+            nc.vector.tensor_tensor(dif[t][:], wins[t][:].indirect(n5_t[:]), cv[t][:], ALU.subtract)
+            nc.scalar.activation(rel[t][:], dif[t][:], ACT.Relu)
+
+        def send(t):
+            dss[t] = keep.tile([P, WIN], F32, name=f"ds{t}")
+            nc.vector.tensor_tensor(dss[t][:].indirect(n4_t[:]), rel[t][:], cv[t][:], ALU.add)
+            nc.scalar.activation(sig[t][:], cv[t][:], ACT.Sigmoid)
+
+        def gate(t, c0, c1):
+            nc.vector.tensor_tensor(res[:, t, c0:c1], dss[t][:, c0:c1], sig[t][:, c0:c1], ALU.mult)
+            nc.sync.dma_start(out_rows[:, t, c0:c1], res[:, t, c0:c1])
+
+        moments(0)
+        moments(1)
+        fetch(0)
+        moments(2)
+        fetch(1)
+        send(0)
+        moments(3)
+        fetch(2)
+        send(1)
+        fetch(3)
+        gate(0, 0, W)
+        send(2)
+        gate(1, 0, W)
+        gate(2, 0, W)
+        send(3)
+        gate(3, 256, 512)
+        gate(3, 0, 256)
+        interleave(nc.scalar.copy, y_mx[0], res[:, :, 256:512], 256, 512)
+        interleave(nc.vector.tensor_copy, y_mx[0], res[:, :, 0:256], 0, 256)
+        words_out = out_1[0].rearrange("p n t -> p (n t)").bitcast(I32)
+        for c0 in (0, 256):
+            quantise(y_mx, c0, c0 + 256)
+            nc.sync.dma_start(words_out[:, c0 : c0 + 256], y_mx[1][:, c0 : c0 + 256])
+        for q in range(4):
+            eng = nc.sync if q % 2 == 0 else nc.scalar
+            eng.dma_start(out_2[0, 4 * q : 4 * q + 4, :].bitcast(I32), y_mx[2][32 * q : 32 * q + 4, :].bitcast(I32))

@@ -42,12 +42,10 @@ def tile_picked_momtop2sendg_none_po_kernel(
         nc.gpsimd.memset(xs[:].bitcast(I32), 0)
         grow = keep.tile([P, P], F32, name="grow")
         nc.gpsimd.memset(grow[:], 0.0)
-        irow = keep.tile([P, P], F32, name="irow")
-        nc.gpsimd.memset(irow[:], 0.0)
 
-        def load_gate(rows, g):
+        def load_gate(r0, g):
             nc.sync.dma_start(
-                rows[0:4, :].rearrange("t (b r) -> t b r", r=8),
+                grow[r0 : r0 + 4, :].rearrange("t (b r) -> t b r", r=8),
                 g.rearrange("(b t r) o -> t b (r o)", t=PACK, r=8),
             )
 
@@ -57,19 +55,19 @@ def tile_picked_momtop2sendg_none_po_kernel(
             return raw
 
         offs_t = load_list(offs, "offs_t")
+        two_t = load_list(two, "two_t")
         wa_raw = [load_weight(wa, "wa_raw0", 0, 256)]
         for q in range(4):
             nc.sync.dma_start(xs[32 * q : 32 * q + 4, :].bitcast(I32), x_scales[0, 4 * q : 4 * q + 4, :].bitcast(I32))
-        two_t = load_list(two, "two_t")
-        load_gate(grow, gt)
         wa_raw.append(load_weight(wa, "wa_raw1", 256, 512))
         xw = keep.tile([P, T], I32, name="xw")
         nc.sync.dma_start(xw[:], x_words[0].rearrange("p n t -> p (n t)").bitcast(I32))
         n1_t = load_list(n1, "n1_t")
         n2_t = load_list(n2, "n2_t")
         n3_t = load_list(n3, "n3_t")
+        load_gate(0, gt)
+        load_gate(4, gi)
         wb_raw = load_weight(wb, "wb_raw", 0, W)
-        load_gate(irow, gi)
         n5_t = load_list(n5, "n5_t")
         n4_t = load_list(n4, "n4_t")
 
@@ -112,7 +110,7 @@ def tile_picked_momtop2sendg_none_po_kernel(
             )
 
         def mx_tiles(name):
-            grouped = keep.tile([P, W, PACK], BF16, name=f"{name}_bf", align_bytes=64)
+            grouped = keep.tile([P, W, PACK], BF16, name=f"{name}_bf", tag=f"{name}_bf", align_bytes=64)
             codes = keep.tile([P, W], I32, name=f"{name}_codes", align_bytes=64)
             scales = keep.tile([P, W], U8, name=f"{name}_scales", align_bytes=64)
             return grouped, codes, scales
@@ -125,14 +123,14 @@ def tile_picked_momtop2sendg_none_po_kernel(
                 in_=grouped[:, c0:c1, :].rearrange("p c t -> p (c t)"),
             )
 
-        def product(acc, words, scales, t, mx):
+        def product(acc, words, scales, t, mx, c0=0, c1=W):
             cols = slice(P * t, P * (t + 1))
             nc.tensor.matmul_mx(
-                out=acc[:],
+                out=acc[:, c0:c1],
                 lhsT=words[:, cols].bitcast(FP8X4),
                 lhsT_scale=scales[:, cols],
-                rhs=mx[1][:].bitcast(FP8X4),
-                rhs_scale=mx[2][:],
+                rhs=mx[1][:, c0:c1].bitcast(FP8X4),
+                rhs_scale=mx[2][:, c0:c1],
                 start=True,
                 stop=True,
             )
@@ -150,27 +148,43 @@ def tile_picked_momtop2sendg_none_po_kernel(
         for h in range(2):
             interleave(nc.scalar.copy, wa_mx[0], wa_raw[h][:], 256 * h, 256 * (h + 1))
             quantise(wa_mx, 256 * h, 256 * (h + 1))
-        gps = psum.tile([P, W], F32, name="u_ps")
-        nc.tensor.transpose(gps[:, 0:P], grow[:], ident[:])
+        xa = pick_words(offs_t, "xa")
         half_abs = keep.tile([P, PACK], F32, name="half_abs")
         sign = keep.tile([P, PACK], F32, name="sign")
         gis = keep.tile([P, PACK], F32, name="gis")
+        gps = psum.tile([P, W], F32, name="b_ps")
+        nc.tensor.transpose(gps[:, 0:P], grow[:], ident[:])
         nc.scalar.activation(half_abs[:], gps[:, 0:4], ACT.Abs, scale=0.5)
         nc.scalar.activation(sign[:], gps[:, 0:4], ACT.Sign)
-
-        xa = pick_words(offs_t, "xa")
-        for t in range(PACK):
-            acc = psum.tile([P, W], F32, name="a_ps")
+        for c0, tag in ((0, "u_ps"), (256, "z_ps")):
+            acc = psum.tile([P, W], F32, name=tag)
+            product(acc, xa, sa, 0, wa_mx, c0, c0 + 256)
+            nc.scalar.activation(wins[0][:, c0 : c0 + 256], acc[:, c0 : c0 + 256], ACT.Copy, scale=half_abs[:, 0:1])
+        for t in range(1, PACK):
+            acc = psum.tile([P, W], F32, name="a_ps" if t < 3 else "b_ps")
             product(acc, xa, sa, t, wa_mx)
             nc.scalar.activation(wins[t][:, :W], acc[:], ACT.Copy, scale=half_abs[:, t : t + 1])
         xb = pick_words(two_t, "xb")
+        nc.vector.tensor_tensor(gis[:], gps[:, 4:8], sign[:], ALU.mult)
 
         zp = keep.tile([P, PACK, W], BF16, name="zp")
         z2p = keep.tile([P, PACK, W], BF16, name="z2p")
         st = {}
 
+        reuse = {("b1", 2): ("x", 0), ("x", 2): ("x", 1), ("b1", 3): ("ax", 1), ("x", 3): ("ax", 2)}
+        for t in range(PACK):
+            st["ax", t] = wb_raw[:, t, :]
+
         def new(name, t):
-            st[name, t] = ring.tile([P, W], F32, name=name)
+            if (name, t) in reuse:
+                st[name, t] = st[reuse[name, t]]
+            elif name == "e" and t < 2:
+                if t == 0:
+                    st["e01"] = keep.tile([P, 2, W], F32, name="e01", tag="wb_bf", align_bytes=64)
+                st[name, t] = st["e01"][:, t, :]
+            elif (name, t) not in st:
+                pool = ring if name in ("x", "b1", "ut") else keep
+                st[name, t] = pool.tile([P, W], F32, name=name if name in ("x", "b1", "ut") else f"{name}{t}")
             return st[name, t]
 
         def sl(part):
@@ -178,23 +192,29 @@ def tile_picked_momtop2sendg_none_po_kernel(
 
         whole = (0, W)
 
-        def step_a(t):
-            nc.vector.tensor_copy(new("b1", t)[:], wins[t][:].indirect(n1_t[:]))
+        def step_a(t, part=(0, W)):
+            c, o = sl(part)
+            nc.vector.tensor_copy(new("b1", t)[:, c], wins[t][:].indirect(n1_t[:, o]))
 
-        def step_b(t):
-            nc.vector.tensor_tensor(new("x", t)[:], wins[t][:].indirect(n2_t[:]), st["b1", t][:], ALU.subtract)
-            nc.scalar.activation(new("ax", t)[:], st["x", t][:], ACT.Abs)
+        def step_b(t, part):
+            c, o = sl(part)
+            nc.vector.tensor_tensor(new("x", t)[:, c], wins[t][:].indirect(n2_t[:, o]), st["b1", t][:, c], ALU.subtract)
 
-        def step_c(t):
-            nc.vector.scalar_tensor_tensor(new("mx", t)[:], st["x", t][:], 0.0, st["b1", t][:], ALU.max, ALU.add)
+        def size_of(t):
+            nc.scalar.activation(st["ax", t][:], st["x", t][:], ACT.Abs)
+
+        def excess(t, part):
+            c, o = sl(part)
+            nc.scalar.activation(new("r", t)[:, c], st["e", t][:, c], ACT.Relu, scale=3.0)
+
+        def step_c(t, part):
+            c, o = sl(part)
+            nc.vector.scalar_tensor_tensor(new("mx", t)[:, c], st["x", t][:, c], 0.0, st["b1", t][:, c], ALU.max, ALU.add)
 
         def step_d(t, part):
             c, o = sl(part)
-            if part[0] == 0:
-                new("e", t)
-                new("r", t)
+            new("e", t)
             nc.vector.tensor_tensor(st["e", t][:, c], wins[t][:].indirect(n3_t[:, o]), st["mx", t][:, c], ALU.subtract)
-            nc.scalar.activation(st["r", t][:, c], st["e", t][:, c], ACT.Relu, scale=3.0)
 
         def step_e(t, part):
             c, o = sl(part)
@@ -206,11 +226,11 @@ def tile_picked_momtop2sendg_none_po_kernel(
             c, o = sl(part)
             if part[0] == 0:
                 new("q", t)
-            nc.vector.tensor_tensor(st["q", t][:, c], st["k", t][:, c], st["mx", t][:, c], ALU.add)
+            nc.vector.scalar_tensor_tensor(st["q", t][:, c], st["k", t][:, c], -2.0, st["k", t][:, c], ALU.mult, ALU.max)
 
         def step_g(t, part):
             c, o = sl(part)
-            nc.vector.tensor_tensor(zp[:, t, c], st["q", t][:, c], st["r", t][:, c], ALU.add)
+            nc.vector.tensor_tensor(zp[:, t, c], st["q", t][:, c], st["mx", t][:, c], ALU.add)
 
         def sum_on_pe(t):
             ups = psum.tile([P, W], F32, name="u_ps")
@@ -221,6 +241,9 @@ def tile_picked_momtop2sendg_none_po_kernel(
                     nc.tensor.matmul(ups[:, c], term[:, c], ident[:], start=(i == 0), stop=(i == 2), is_transpose=True)
             ut = new("ut", t)
             nc.scalar.copy(ut[:], ups[:])
+
+        def turn_back(t):
+            ut = st["ut", t]
             zps = psum.tile([P, W], F32, name="z_ps")
             for q in range(4):
                 c = slice(P * q, P * (q + 1))
@@ -229,66 +252,64 @@ def tile_picked_momtop2sendg_none_po_kernel(
 
         def finish(t):
             step_e(t, whole)
-            if t < NPE:
-                sum_on_pe(t)
-
-        def finish2(t):
-            if t >= NPE:
-                step_f(t, whole)
-
-        def finish3(t):
-            if t >= NPE:
-                step_g(t, whole)
+            sum_on_pe(t)
 
         def b_weights():
             for h in range(2):
                 interleave(nc.scalar.copy, wb_mx[0], wb_raw[:, :, 256 * h : 256 * (h + 1)], 256 * h, 256 * (h + 1))
-            ips = psum.tile([P, W], F32, name="z_ps")
-            nc.tensor.transpose(ips[:, 0:P], irow[:], ident[:])
-            nc.vector.tensor_tensor(gis[:], ips[:, 0:4], sign[:], ALU.mult)
 
         def b_product():
             quantise(wb_mx, 0, W)
             for t in range(PACK):
-                acc = psum.tile([P, W], F32, name="b_ps")
+                acc = psum.tile([P, W], F32, name="b_ps" if t < 2 else "z_ps")
                 product(acc, xb, sb, t, wb_mx)
                 nc.scalar.activation(z2p[:, t, :], acc[:], ACT.Copy, scale=gis[:, t : t + 1])
 
         def b_group(h):
             interleave(nc.scalar.copy, z2_mx[0], z2p[:, :, 256 * h : 256 * (h + 1)], 256 * h, 256 * (h + 1))
 
-        step_a(0)
-        step_a(1)
-        step_b(0)
-        step_b(1)
-        b_weights()
-        step_c(0)
-        step_a(2)
-        step_d(0, whole)
-        step_c(1)
-        finish(0)
-        step_d(1, whole)
-        finish2(0)
-        b_product()
-        step_b(2)
-        finish3(0)
-        finish(1)
-        step_c(2)
-        finish2(1)
-        step_a(3)
-        finish3(1)
-        b_group(0)
-        step_d(2, whole)
-        step_b(3)
-        finish(2)
-        b_group(1)
-        step_c(3)
-        finish2(2)
         halves = [(0, 256), (256, 512)]
-        step_d(3, halves[0])
-        finish3(2)
-        step_d(3, halves[1])
+        b_weights()
+        step_a(0, halves[0])
+        step_a(0, halves[1])
+        step_a(1)
+        step_b(0, halves[0])
+        step_b(0, halves[1])
+        step_b(1, whole)
+        size_of(0)
+        size_of(1)
+        step_c(0, whole)
+        b_product()
+        step_c(1, whole)
+        step_d(0, whole)
+        step_d(1, whole)
+        excess(0, whole)
+        excess(1, whole)
+        b_group(0)
+        step_a(2)
+        step_e(0, whole)
+        step_b(2, whole)
+        size_of(2)
+        sum_on_pe(0)
+        b_group(1)
+        step_e(1, whole)
+        turn_back(0)
+        sum_on_pe(1)
+        step_c(2, whole)
+        step_a(3)
+        step_d(2, whole)
+        excess(2, whole)
+        turn_back(1)
         quantise(z2_mx, 0, W)
+        step_e(2, whole)
+        for part in halves:
+            step_b(3, part)
+        size_of(3)
+        sum_on_pe(2)
+        for step in (step_c, step_d):
+            for part in halves:
+                step(3, part)
+        turn_back(2)
         for step in (step_e, step_f, step_g):
             for part in halves:
                 step(3, part)
@@ -301,10 +322,10 @@ def tile_picked_momtop2sendg_none_po_kernel(
 
         z_group(nc.vector.tensor_copy, 0)
         z_group(nc.scalar.copy, 1)
-        quantise(z_mx, 0, 128)
+        z_group(nc.scalar.copy, 3)
         z_group(nc.vector.tensor_copy, 2)
+        quantise(z_mx, 0, 128)
         quantise(z_mx, 128, 256)
-        z_group(nc.vector.tensor_copy, 3)
         quantise(z_mx, 256, 512)
 
         out_rows = out_0.rearrange("(p t) c -> p t c", t=PACK)
@@ -328,33 +349,55 @@ def tile_picked_momtop2sendg_none_po_kernel(
         def send(t):
             dss[t] = keep.tile([P, WIN], F32, name=f"ds{t}")
             nc.vector.tensor_tensor(dss[t][:].indirect(n4_t[:]), rel[t][:], cv[t][:], ALU.add)
+
+        def squash(t):
             nc.scalar.activation(sig[t][:], cv[t][:], ACT.Sigmoid)
 
         def gate(t, c0, c1):
             nc.vector.tensor_tensor(res[:, t, c0:c1], dss[t][:, c0:c1], sig[t][:, c0:c1], ALU.mult)
             nc.sync.dma_start(out_rows[:, t, c0:c1], res[:, t, c0:c1])
 
-        moments(0)
+        def pair(engine_copy, t0, c0, c1):
+            engine_copy(
+                y_mx[0][:, c0:c1, t0 : t0 + 2].rearrange("p (c i) t -> p c i t", i=4),
+                res[:, t0 : t0 + 2, c0:c1].rearrange("p t (c i) -> p c i t", i=4),
+            )
+
+        cv[0] = keep.tile([P, W], F32, name="cv0")
+        sig[0] = keep.tile([P, W], F32, name="sig0")
+        lo = psum.tile([P, W], F32, name="a_ps")
+        hi = psum.tile([P, W], F32, name="u_ps")
+        product(lo, z_mx[1], z_mx[2], 0, z2_mx, 0, 256)
+        product(hi, z_mx[1], z_mx[2], 0, z2_mx, 256, 512)
+        for dst in (wins[0], cv[0]):
+            nc.scalar.activation(dst[:, 0:256], lo[:, 0:256], ACT.Copy, scale=0.0625)
+            nc.vector.tensor_scalar_mul(dst[:, 256:512], hi[:, 256:512], 0.0625)
         moments(1)
         fetch(0)
         moments(2)
         fetch(1)
         send(0)
+        squash(0)
         moments(3)
         fetch(2)
         send(1)
+        squash(1)
+        squash(2)
         fetch(3)
+        squash(3)
         gate(0, 0, W)
         send(2)
         gate(1, 0, W)
+        pair(nc.scalar.copy, 0, 0, W)
         gate(2, 0, W)
         send(3)
         gate(3, 256, 512)
         gate(3, 0, 256)
-        interleave(nc.scalar.copy, y_mx[0], res[:, :, 256:512], 256, 512)
-        interleave(nc.vector.tensor_copy, y_mx[0], res[:, :, 0:256], 0, 256)
+        pair(nc.scalar.copy, 2, 384, 512)
+        pair(nc.vector.tensor_copy, 2, 256, 384)
+        pair(nc.vector.tensor_copy, 2, 0, 256)
         words_out = out_1[0].rearrange("p n t -> p (n t)").bitcast(I32)
-        for c0 in (0, 256):
+        for c0 in (256, 0):
             quantise(y_mx, c0, c0 + 256)
             nc.sync.dma_start(words_out[:, c0 : c0 + 256], y_mx[1][:, c0 : c0 + 256])
         for q in range(4):

@@ -3,7 +3,6 @@ from contextlib import ExitStack
 import concourse.mybir as mybir
 from concourse.masks import make_identity
 
-K, T, S, H, N = 512, 2048, 512, 512, 512
 FLOPS = 3 * 2 * 512 * 512 * 512
 
 F32 = mybir.dt.float32
@@ -18,9 +17,19 @@ ACT = mybir.ActivationFunctionType
 
 P = 128
 PACK = 4
+TOKENS = 2048
 W = 512
-WIN = 1024
-NPE = 3
+HALF = W // 2
+WINDOW = 2 * W
+LAST = PACK - 1
+CV_SCALE = 0.0625
+WHOLE = slice(0, W)
+HALVES = (slice(0, HALF), slice(HALF, W))
+BLOCKS = tuple(slice(P * q, P * (q + 1)) for q in range(W // P))
+
+
+def entries(cols):
+    return slice(cols.start // 16, cols.stop // 16)
 
 
 def tile_picked_momtop2sendg_none_po_kernel(
@@ -33,41 +42,46 @@ def tile_picked_momtop2sendg_none_po_kernel(
         ring = ctx.enter_context(tc.tile_pool(name="ring", bufs=2))
         psum = ctx.enter_context(tc.psum_pool(name="psum", bufs=2))
 
+        def plane(name):
+            return keep.tile([P, W], F32, name=name)
+
+        def bank(tag):
+            return psum.tile([P, W], F32, name=tag)
+
         def load_list(src, name):
             tile = lists.tile([P, W // 16], U16, name=name)
             nc.sync.dma_start(tile[:], src)
             return tile
 
-        xs = keep.tile([P, T], U8, name="xs")
-        nc.gpsimd.memset(xs[:].bitcast(I32), 0)
-        grow = keep.tile([P, P], F32, name="grow")
-        nc.gpsimd.memset(grow[:], 0.0)
-
-        def load_gate(r0, g):
-            nc.sync.dma_start(
-                grow[r0 : r0 + 4, :].rearrange("t (b r) -> t b r", r=8),
-                g.rearrange("(b t r) o -> t b (r o)", t=PACK, r=8),
-            )
-
-        def load_weight(w, name, c0, c1):
-            raw = keep.tile([P, PACK, c1 - c0], F32, name=name)
-            nc.sync.dma_start(raw[:], w.rearrange("(p j) c -> p j c", j=PACK)[:, :, c0:c1])
+        def load_weight(w, name, cols):
+            raw = keep.tile([P, PACK, cols.stop - cols.start], F32, name=name)
+            nc.sync.dma_start(raw[:], w.rearrange("(p j) c -> p j c", j=PACK)[:, :, cols])
             return raw
+
+        x_scale_rows = keep.tile([P, TOKENS], U8, name="x_scale_rows")
+        nc.gpsimd.memset(x_scale_rows[:].bitcast(I32), 0)
+        gate_rows = keep.tile([P, P], F32, name="gate_rows")
+        nc.gpsimd.memset(gate_rows[:], 0.0)
 
         offs_t = load_list(offs, "offs_t")
         two_t = load_list(two, "two_t")
-        wa_raw = [load_weight(wa, "wa_raw0", 0, 256)]
+        wa_raw = [load_weight(wa, "wa_raw0", HALVES[0])]
         for q in range(4):
-            nc.sync.dma_start(xs[32 * q : 32 * q + 4, :].bitcast(I32), x_scales[0, 4 * q : 4 * q + 4, :].bitcast(I32))
-        wa_raw.append(load_weight(wa, "wa_raw1", 256, 512))
-        xw = keep.tile([P, T], I32, name="xw")
-        nc.sync.dma_start(xw[:], x_words[0].rearrange("p n t -> p (n t)").bitcast(I32))
+            nc.sync.dma_start(
+                x_scale_rows[32 * q : 32 * q + 4, :].bitcast(I32), x_scales[0, 4 * q : 4 * q + 4, :].bitcast(I32)
+            )
+        wa_raw.append(load_weight(wa, "wa_raw1", HALVES[1]))
+        x_word_rows = keep.tile([P, TOKENS], I32, name="x_word_rows")
+        nc.sync.dma_start(x_word_rows[:], x_words[0].rearrange("p n t -> p (n t)").bitcast(I32))
         n1_t = load_list(n1, "n1_t")
         n2_t = load_list(n2, "n2_t")
         n3_t = load_list(n3, "n3_t")
-        load_gate(0, gt)
-        load_gate(4, gi)
-        wb_raw = load_weight(wb, "wb_raw", 0, W)
+        for first_row, gate_in in ((0, gt), (PACK, gi)):
+            nc.sync.dma_start(
+                gate_rows[first_row : first_row + PACK, :].rearrange("t (b r) -> t b r", r=8),
+                gate_in.rearrange("(b t r) o -> t b (r o)", t=PACK, r=8),
+            )
+        wb_raw = load_weight(wb, "wb_raw", WHOLE)
         n5_t = load_list(n5, "n5_t")
         n4_t = load_list(n4, "n4_t")
 
@@ -76,330 +90,290 @@ def tile_picked_momtop2sendg_none_po_kernel(
         warm = keep.tile([P, 1], F32, name="warm")
         nc.scalar.activation(warm[:], ident[:, 0:1], ACT.Sigmoid)
 
-        wins = []
+        windows = []
         for t in range(PACK):
-            win = keep.tile([P, WIN], F32, name=f"win{t}")
-            nc.gpsimd.memset(win[:, W:], 0.0)
-            wins.append(win)
+            window = keep.tile([P, WINDOW], F32, name=f"window{t}")
+            nc.gpsimd.memset(window[:, W:], 0.0)
+            windows.append(window)
 
-        def pick_scales(lst, name):
-            plain = keep.tile([P, W], U8, name=f"{name}_plain", align_bytes=64)
-            nc.vector.tensor_copy(plain[:], xs[:].indirect(lst[:]))
-            return plain
-
-        def deal_scales(plain, name):
-            dealt = keep.tile([P, W], U8, name=f"{name}_dealt", align_bytes=64)
-            nc.vector.tensor_copy(
-                dealt[:].bitcast(I32).rearrange("p (t b r) -> p b t r", t=PACK, r=2),
-                plain[:].bitcast(I32).rearrange("p (b t r) -> p b t r", t=PACK, r=2),
-            )
-            return dealt
-
-        def pick_words(lst, name):
+        def mx_operand(name):
+            values = keep.tile([P, W, PACK], BF16, name=f"{name}_values", tag=f"{name}_values", align_bytes=64)
             words = keep.tile([P, W], I32, name=f"{name}_words", align_bytes=64)
-            nc.vector.tensor_copy(
-                words[:].bitcast(U32).rearrange("p (t b r) -> p b t r", t=PACK, r=8),
-                xw[:].bitcast(U32).indirect(lst[:]),
-            )
-            return words
-
-        def interleave(engine_copy, dst, src, c0, c1):
-            engine_copy(
-                dst[:, c0:c1, :].rearrange("p (c i) t -> p c t i", i=4),
-                src.rearrange("p t (c i) -> p c t i", i=4),
-            )
-
-        def mx_tiles(name):
-            grouped = keep.tile([P, W, PACK], BF16, name=f"{name}_bf", tag=f"{name}_bf", align_bytes=64)
-            codes = keep.tile([P, W], I32, name=f"{name}_codes", align_bytes=64)
             scales = keep.tile([P, W], U8, name=f"{name}_scales", align_bytes=64)
-            return grouped, codes, scales
+            return values, words, scales
 
-        def quantise(mx, c0, c1):
-            grouped, codes, scales = mx
-            nc.vector.quantize_mx(
-                out=codes[:, c0:c1].bitcast(FP8X4),
-                scales=scales[:, c0:c1],
-                in_=grouped[:, c0:c1, :].rearrange("p c t -> p (c t)"),
+        def interleave(mx, src, cols):
+            nc.scalar.copy(
+                mx[0][:, cols, :].rearrange("p (c i) j -> p c j i", i=4),
+                src.rearrange("p j (c i) -> p c j i", i=4),
             )
 
-        def product(acc, words, scales, t, mx, c0=0, c1=W):
-            cols = slice(P * t, P * (t + 1))
+        def quantise(mx, cols):
+            values, words, scales = mx
+            nc.vector.quantize_mx(
+                out=words[:, cols].bitcast(FP8X4),
+                scales=scales[:, cols],
+                in_=values[:, cols, :].rearrange("p c j -> p (c j)"),
+            )
+
+        def product(acc, left, t, right, cols):
             nc.tensor.matmul_mx(
-                out=acc[:, c0:c1],
-                lhsT=words[:, cols].bitcast(FP8X4),
-                lhsT_scale=scales[:, cols],
-                rhs=mx[1][:, c0:c1].bitcast(FP8X4),
-                rhs_scale=mx[2][:, c0:c1],
+                out=acc[:, cols],
+                lhsT=left[1][:, BLOCKS[t]].bitcast(FP8X4),
+                lhsT_scale=left[2][:, BLOCKS[t]],
+                rhs=right[1][:, cols].bitcast(FP8X4),
+                rhs_scale=right[2][:, cols],
                 start=True,
                 stop=True,
             )
 
-        wa_mx = mx_tiles("wa")
-        wb_mx = mx_tiles("wb")
-        z_mx = mx_tiles("z")
-        z2_mx = mx_tiles("z2")
-        y_mx = mx_tiles("y")
-
-        sa_plain = pick_scales(offs_t, "sa")
-        sb_plain = pick_scales(two_t, "sb")
-        sa = deal_scales(sa_plain, "sa")
-        sb = deal_scales(sb_plain, "sb")
-        for h in range(2):
-            interleave(nc.scalar.copy, wa_mx[0], wa_raw[h][:], 256 * h, 256 * (h + 1))
-            quantise(wa_mx, 256 * h, 256 * (h + 1))
-        xa = pick_words(offs_t, "xa")
-        half_abs = keep.tile([P, PACK], F32, name="half_abs")
-        sign = keep.tile([P, PACK], F32, name="sign")
-        gis = keep.tile([P, PACK], F32, name="gis")
-        gps = psum.tile([P, W], F32, name="b_ps")
-        nc.tensor.transpose(gps[:, 0:P], grow[:], ident[:])
-        nc.scalar.activation(half_abs[:], gps[:, 0:4], ACT.Abs, scale=0.5)
-        nc.scalar.activation(sign[:], gps[:, 0:4], ACT.Sign)
-        for c0, tag in ((0, "u_ps"), (256, "z_ps")):
-            acc = psum.tile([P, W], F32, name=tag)
-            product(acc, xa, sa, 0, wa_mx, c0, c0 + 256)
-            nc.scalar.activation(wins[0][:, c0 : c0 + 256], acc[:, c0 : c0 + 256], ACT.Copy, scale=half_abs[:, 0:1])
-        for t in range(1, PACK):
-            acc = psum.tile([P, W], F32, name="a_ps" if t < 3 else "b_ps")
-            product(acc, xa, sa, t, wa_mx)
-            nc.scalar.activation(wins[t][:, :W], acc[:], ACT.Copy, scale=half_abs[:, t : t + 1])
-        xb = pick_words(two_t, "xb")
-        nc.vector.tensor_tensor(gis[:], gps[:, 4:8], sign[:], ALU.mult)
-
-        zp = keep.tile([P, PACK, W], BF16, name="zp")
-        z2p = keep.tile([P, PACK, W], BF16, name="z2p")
-        st = {}
-
-        reuse = {("b1", 2): ("x", 0), ("x", 2): ("x", 1), ("b1", 3): ("ax", 1), ("x", 3): ("ax", 2)}
-        for t in range(PACK):
-            st["ax", t] = wb_raw[:, t, :]
-
-        def new(name, t):
-            if (name, t) in reuse:
-                st[name, t] = st[reuse[name, t]]
-            elif name == "e" and t < 2:
-                if t == 0:
-                    st["e01"] = keep.tile([P, 2, W], F32, name="e01", tag="wb_bf", align_bytes=64)
-                st[name, t] = st["e01"][:, t, :]
-            elif (name, t) not in st:
-                pool = ring if name in ("x", "b1", "ut") else keep
-                st[name, t] = pool.tile([P, W], F32, name=name if name in ("x", "b1", "ut") else f"{name}{t}")
-            return st[name, t]
-
-        def sl(part):
-            return slice(part[0], part[1]), slice(part[0] // 16, part[1] // 16)
-
-        whole = (0, W)
-
-        def step_a(t, part=(0, W)):
-            c, o = sl(part)
-            nc.vector.tensor_copy(new("b1", t)[:, c], wins[t][:].indirect(n1_t[:, o]))
-
-        def step_b(t, part):
-            c, o = sl(part)
-            nc.vector.tensor_tensor(new("x", t)[:, c], wins[t][:].indirect(n2_t[:, o]), st["b1", t][:, c], ALU.subtract)
-
-        def size_of(t):
-            nc.scalar.activation(st["ax", t][:], st["x", t][:], ACT.Abs)
-
-        def excess(t, part):
-            c, o = sl(part)
-            nc.scalar.activation(new("r", t)[:, c], st["e", t][:, c], ACT.Relu, scale=3.0)
-
-        def step_c(t, part):
-            c, o = sl(part)
-            nc.vector.scalar_tensor_tensor(new("mx", t)[:, c], st["x", t][:, c], 0.0, st["b1", t][:, c], ALU.max, ALU.add)
-
-        def step_d(t, part):
-            c, o = sl(part)
-            new("e", t)
-            nc.vector.tensor_tensor(st["e", t][:, c], wins[t][:].indirect(n3_t[:, o]), st["mx", t][:, c], ALU.subtract)
-
-        def step_e(t, part):
-            c, o = sl(part)
-            if part[0] == 0:
-                new("k", t)
-            nc.vector.scalar_tensor_tensor(st["k", t][:, c], st["e", t][:, c], -1.0, st["ax", t][:, c], ALU.mult, ALU.min)
-
-        def step_f(t, part):
-            c, o = sl(part)
-            if part[0] == 0:
-                new("q", t)
-            nc.vector.scalar_tensor_tensor(st["q", t][:, c], st["k", t][:, c], -2.0, st["k", t][:, c], ALU.mult, ALU.max)
-
-        def step_g(t, part):
-            c, o = sl(part)
-            nc.vector.tensor_tensor(zp[:, t, c], st["q", t][:, c], st["mx", t][:, c], ALU.add)
-
-        def sum_on_pe(t):
-            ups = psum.tile([P, W], F32, name="u_ps")
-            terms = [st["mx", t], st["r", t], st["k", t]]
-            for q in range(4):
-                c = slice(P * q, P * (q + 1))
+        def add_turned(tag, terms):
+            acc = bank(tag)
+            for cols in BLOCKS:
                 for i, term in enumerate(terms):
-                    nc.tensor.matmul(ups[:, c], term[:, c], ident[:], start=(i == 0), stop=(i == 2), is_transpose=True)
-            ut = new("ut", t)
-            nc.scalar.copy(ut[:], ups[:])
+                    nc.tensor.matmul(
+                        acc[:, cols], term[:, cols], ident[:],
+                        start=(i == 0), stop=(i == len(terms) - 1), is_transpose=True,
+                    )
+            return acc
+
+        def pick_scales(offsets, name):
+            picked = keep.tile([P, W], U8, name=name, align_bytes=64)
+            nc.vector.tensor_copy(picked[:], x_scale_rows[:].indirect(offsets[:]))
+            return picked
+
+        def deal_scales(picked, name):
+            dealt = keep.tile([P, W], U8, name=name, align_bytes=64)
+            nc.vector.tensor_copy(
+                dealt[:].bitcast(I32).rearrange("p (t b r) -> p b t r", t=PACK, r=2),
+                picked[:].bitcast(I32).rearrange("p (b t r) -> p b t r", t=PACK, r=2),
+            )
+            return dealt
+
+        def pick_words(offsets, name):
+            words = keep.tile([P, W], I32, name=name, align_bytes=64)
+            nc.vector.tensor_copy(
+                words[:].bitcast(U32).rearrange("p (t b r) -> p b t r", t=PACK, r=8),
+                x_word_rows[:].bitcast(U32).indirect(offsets[:]),
+            )
+            return words
+
+        wa_mx, wb_mx, z_mx, z2_mx, out_mx = (mx_operand(name) for name in ("wa", "wb", "z", "z2", "out"))
+
+        xa_picked = pick_scales(offs_t, "xa_picked")
+        xb_picked = pick_scales(two_t, "xb_picked")
+        xa_scales = deal_scales(xa_picked, "xa_scales")
+        xb_scales = deal_scales(xb_picked, "xb_scales")
+        for raw, cols in zip(wa_raw, HALVES):
+            interleave(wa_mx, raw[:], cols)
+            quantise(wa_mx, cols)
+        xa_mx = (None, pick_words(offs_t, "xa_words"), xa_scales)
+
+        for cols, tag in zip(HALVES, ("sum_ps", "back_ps")):
+            acc = bank(tag)
+            product(acc, xa_mx, 0, wa_mx, cols)
+            nc.scalar.copy(windows[0][:, cols], acc[:, cols])
+        for t in range(1, LAST):
+            acc = bank("a_ps")
+            product(acc, xa_mx, t, wa_mx, WHOLE)
+            nc.scalar.copy(windows[t][:, WHOLE], acc[:])
+        a_last = bank("b_ps")
+        product(a_last, xa_mx, LAST, wa_mx, WHOLE)
+
+        gates = bank("b_ps")
+        nc.tensor.transpose(gates[:, 0:P], gate_rows[:], ident[:])
+        half_size = keep.tile([P, PACK], F32, name="half_size")
+        sign = keep.tile([P, PACK], F32, name="sign")
+        signed_gi = keep.tile([P, PACK], F32, name="signed_gi")
+        nc.scalar.activation(half_size[:], gates[:, 0:PACK], ACT.Abs, scale=0.5)
+        nc.scalar.activation(sign[:], gates[:, 0:PACK], ACT.Sign)
+        nc.scalar.activation(windows[LAST][:, WHOLE], a_last[:], ACT.Copy, scale=half_size[:, LAST : LAST + 1])
+        xb_mx = (None, pick_words(two_t, "xb_words"), xb_scales)
+
+        z_planes = keep.tile([P, PACK, W], BF16, name="z_planes")
+        z2_planes = keep.tile([P, PACK, W], BF16, name="z2_planes")
+        size = [wb_raw[:, t, :] for t in range(PACK)]
+        x01 = [plane("x0"), plane("x1")]
+        b1 = [plane("b1_0"), plane("b1_1"), x01[0], size[2]]
+        x = [x01[0], x01[1], x01[1], size[1]]
+        top = [plane(f"top{t}") for t in range(PACK)]
+        k = [plane(f"k{t}") for t in range(PACK)]
+        rest = [plane(f"rest{t}") for t in range(PACK)]
+        e = {t: plane(f"e{t}") for t in (2, LAST)}
+        turned = {}
+
+        def fetch_b1(t, cols):
+            nc.vector.tensor_copy(b1[t][:, cols], windows[t][:].indirect(n1_t[:, entries(cols)]))
+
+        def fetch_x(t, cols):
+            nc.vector.tensor_tensor(
+                x[t][:, cols], windows[t][:].indirect(n2_t[:, entries(cols)]), b1[t][:, cols], ALU.subtract
+            )
+
+        def make_size(t):
+            nc.scalar.activation(size[t][:, WHOLE], x[t][:, WHOLE], ACT.Abs)
+
+        def make_top(t, cols):
+            nc.vector.scalar_tensor_tensor(top[t][:, cols], x[t][:, cols], 0.0, b1[t][:, cols], ALU.max, ALU.add)
+
+        def fetch_e(t, cols):
+            nc.vector.tensor_tensor(
+                e[t][:, cols], windows[t][:].indirect(n3_t[:, entries(cols)]), top[t][:, cols], ALU.subtract
+            )
+
+        def make_k(t, cols):
+            nc.vector.scalar_tensor_tensor(k[t][:, cols], e[t][:, cols], -1.0, size[t][:, cols], ALU.mult, ALU.min)
+
+        def make_excess(t):
+            nc.scalar.activation(rest[t][:], e[t][:, WHOLE], ACT.Relu, scale=3.0)
+
+        def add_up(t):
+            turned[t] = ring.tile([P, W], F32, name="turned")
+            nc.scalar.copy(turned[t][:], add_turned("sum_ps", [top[t], rest[t], k[t]])[:])
 
         def turn_back(t):
-            ut = st["ut", t]
-            zps = psum.tile([P, W], F32, name="z_ps")
-            for q in range(4):
-                c = slice(P * q, P * (q + 1))
-                nc.tensor.transpose(zps[:, c], ut[:, c], ident[:])
-            nc.scalar.copy(zp[:, t, :], zps[:])
+            acc = add_turned("back_ps", [turned[t]])
+            nc.scalar.activation(z_planes[:, t, :], acc[:], ACT.Copy, scale=half_size[:, t : t + 1])
 
-        def finish(t):
-            step_e(t, whole)
-            sum_on_pe(t)
+        def fold_k(t, cols):
+            nc.vector.scalar_tensor_tensor(rest[t][:, cols], k[t][:, cols], -2.0, k[t][:, cols], ALU.mult, ALU.max)
 
-        def b_weights():
-            for h in range(2):
-                interleave(nc.scalar.copy, wb_mx[0], wb_raw[:, :, 256 * h : 256 * (h + 1)], 256 * h, 256 * (h + 1))
+        def add_top(t, cols):
+            nc.vector.tensor_tensor(z_planes[:, t, cols], rest[t][:, cols], top[t][:, cols], ALU.add)
 
-        def b_product():
-            quantise(wb_mx, 0, W)
-            for t in range(PACK):
-                acc = psum.tile([P, W], F32, name="b_ps" if t < 2 else "z_ps")
-                product(acc, xb, sb, t, wb_mx)
-                nc.scalar.activation(z2p[:, t, :], acc[:], ACT.Copy, scale=gis[:, t : t + 1])
+        def in_halves(t, steps):
+            for step in steps:
+                for cols in HALVES:
+                    step(t, cols)
 
-        def b_group(h):
-            interleave(nc.scalar.copy, z2_mx[0], z2p[:, :, 256 * h : 256 * (h + 1)], 256 * h, 256 * (h + 1))
-
-        halves = [(0, 256), (256, 512)]
-        b_weights()
-        step_a(0, halves[0])
-        step_a(0, halves[1])
-        step_a(1)
-        step_b(0, halves[0])
-        step_b(0, halves[1])
-        step_b(1, whole)
-        size_of(0)
-        size_of(1)
-        step_c(0, whole)
-        b_product()
-        step_c(1, whole)
-        step_d(0, whole)
-        step_d(1, whole)
-        excess(0, whole)
-        excess(1, whole)
-        b_group(0)
-        step_a(2)
-        step_e(0, whole)
-        step_b(2, whole)
-        size_of(2)
-        sum_on_pe(0)
-        b_group(1)
-        step_e(1, whole)
+        for cols in HALVES:
+            interleave(wb_mx, wb_raw[:, :, cols], cols)
+        in_halves(0, (fetch_b1,))
+        fetch_x(0, HALVES[0])
+        fetch_b1(1, WHOLE)
+        fetch_x(0, HALVES[1])
+        fetch_x(1, WHOLE)
+        make_size(0)
+        make_size(1)
+        make_top(0, WHOLE)
+        quantise(wb_mx, WHOLE)
+        nc.vector.tensor_tensor(signed_gi[:], gates[:, PACK : 2 * PACK], sign[:], ALU.mult)
+        for t, tag in enumerate(("b_ps", "b_ps", "back_ps", "back_ps")):
+            acc = bank(tag)
+            product(acc, xb_mx, t, wb_mx, WHOLE)
+            nc.scalar.activation(z2_planes[:, t, :], acc[:], ACT.Copy, scale=signed_gi[:, t : t + 1])
+        e01 = keep.tile([P, 2, W], F32, name="e01", tag="wb_values", align_bytes=64)
+        e.update({t: e01[:, t, :] for t in (0, 1)})
+        make_top(1, WHOLE)
+        fetch_e(0, WHOLE)
+        fetch_e(1, WHOLE)
+        make_excess(0)
+        make_excess(1)
+        interleave(z2_mx, z2_planes[:, :, HALVES[0]], HALVES[0])
+        fetch_b1(2, WHOLE)
+        make_k(0, WHOLE)
+        fetch_x(2, WHOLE)
+        make_size(2)
+        add_up(0)
+        make_k(1, WHOLE)
+        in_halves(2, (make_top, fetch_e, make_k))
+        interleave(z2_mx, z2_planes[:, :, HALVES[1]], HALVES[1])
+        make_excess(2)
         turn_back(0)
-        sum_on_pe(1)
-        step_c(2, whole)
-        step_a(3)
-        step_d(2, whole)
-        excess(2, whole)
+        add_up(1)
+        in_halves(LAST, (fetch_b1, fetch_x))
+        add_up(2)
+        make_size(LAST)
         turn_back(1)
-        quantise(z2_mx, 0, W)
-        step_e(2, whole)
-        for part in halves:
-            step_b(3, part)
-        size_of(3)
-        sum_on_pe(2)
-        for step in (step_c, step_d):
-            for part in halves:
-                step(3, part)
         turn_back(2)
-        for step in (step_e, step_f, step_g):
-            for part in halves:
-                step(3, part)
+        quantise(z2_mx, WHOLE)
+        in_halves(LAST, (make_top, fetch_e, make_k, fold_k, add_top))
 
-        def z_group(engine_copy, u):
+        z_dealt = z_planes[:].rearrange("p t (m u) -> p u m t", u=PACK)
+
+        def group_z(engine_copy, u, first, last):
+            engine_copy(z_mx[0][:, P * u + first : P * u + last, :], z_dealt[:, u, first:last])
+
+        group_z(nc.vector.tensor_copy, 0, 0, P // 2)
+        group_z(nc.vector.tensor_copy, 0, P // 2, P)
+        group_z(nc.scalar.copy, 1, 0, P)
+        group_z(nc.scalar.copy, 2, 0, P)
+        quantise(z_mx, BLOCKS[0])
+        group_z(nc.vector.tensor_copy, 3, 0, P)
+        quantise(z_mx, BLOCKS[1])
+        quantise(z_mx, HALVES[1])
+
+        out_rows = out_0.rearrange("(p u) c -> p u c", u=PACK)
+        result = keep.tile([P, PACK, W], F32, name="result")
+        sent = [keep.tile([P, WINDOW], F32, name=f"sent{u}") for u in range(PACK)]
+        squashed = [plane(f"squashed{u}") for u in range(PACK)]
+        gap = [plane(f"gap{u}") for u in range(PACK)]
+        rise = [plane(f"rise{u}") for u in range(PACK)]
+
+        def group_out(engine_copy, u, cols):
             engine_copy(
-                z_mx[0][:, P * u : P * (u + 1), :],
-                zp[:].rearrange("p t (m u) -> p u m t", u=4)[:, u],
+                out_mx[0][:, cols, u : u + 2].rearrange("p (c i) j -> p c i j", i=4),
+                result[:, u : u + 2, cols].rearrange("p j (c i) -> p c i j", i=4),
             )
+        cv = [plane(f"cv{u}") for u in range(PACK)]
 
-        z_group(nc.vector.tensor_copy, 0)
-        z_group(nc.scalar.copy, 1)
-        z_group(nc.scalar.copy, 3)
-        z_group(nc.vector.tensor_copy, 2)
-        quantise(z_mx, 0, 128)
-        quantise(z_mx, 128, 256)
-        quantise(z_mx, 256, 512)
+        def make_cv(u, tag):
+            acc = bank(tag)
+            product(acc, z_mx, u, z2_mx, WHOLE)
+            for dst in (windows[u], cv[u]):
+                nc.scalar.activation(dst[:, WHOLE], acc[:], ACT.Copy, scale=CV_SCALE)
 
-        out_rows = out_0.rearrange("(p t) c -> p t c", t=PACK)
-        res = keep.tile([P, PACK, W], F32, name="res")
-        cv, sig, dif, rel, dss = {}, {}, {}, {}, {}
+        def fetch(u):
+            nc.vector.tensor_tensor(gap[u][:], windows[u][:].indirect(n5_t[:]), cv[u][:], ALU.subtract)
+            nc.scalar.activation(rise[u][:], gap[u][:], ACT.Relu)
 
-        def moments(t):
-            acc = psum.tile([P, W], F32, name="a_ps" if t % 2 == 0 else "b_ps")
-            product(acc, z_mx[1], z_mx[2], t, z2_mx)
-            cv[t] = keep.tile([P, W], F32, name=f"cv{t}")
-            sig[t] = keep.tile([P, W], F32, name=f"sig{t}")
-            nc.scalar.activation(wins[t][:, :W], acc[:], ACT.Copy, scale=0.0625)
-            nc.scalar.activation(cv[t][:], acc[:], ACT.Copy, scale=0.0625)
+        def send(u):
+            nc.vector.tensor_tensor(sent[u][:].indirect(n4_t[:]), rise[u][:], cv[u][:], ALU.add)
 
-        def fetch(t):
-            dif[t] = keep.tile([P, W], F32, name=f"dif{t}")
-            rel[t] = keep.tile([P, W], F32, name=f"rel{t}")
-            nc.vector.tensor_tensor(dif[t][:], wins[t][:].indirect(n5_t[:]), cv[t][:], ALU.subtract)
-            nc.scalar.activation(rel[t][:], dif[t][:], ACT.Relu)
+        def squash(u):
+            nc.scalar.activation(squashed[u][:], cv[u][:], ACT.Sigmoid)
 
-        def send(t):
-            dss[t] = keep.tile([P, WIN], F32, name=f"ds{t}")
-            nc.vector.tensor_tensor(dss[t][:].indirect(n4_t[:]), rel[t][:], cv[t][:], ALU.add)
+        def gate(u, cols):
+            nc.vector.tensor_tensor(result[:, u, cols], sent[u][:, cols], squashed[u][:, cols], ALU.mult)
+            nc.sync.dma_start(out_rows[:, u, cols], result[:, u, cols])
 
-        def squash(t):
-            nc.scalar.activation(sig[t][:], cv[t][:], ACT.Sigmoid)
-
-        def gate(t, c0, c1):
-            nc.vector.tensor_tensor(res[:, t, c0:c1], dss[t][:, c0:c1], sig[t][:, c0:c1], ALU.mult)
-            nc.sync.dma_start(out_rows[:, t, c0:c1], res[:, t, c0:c1])
-
-        def pair(engine_copy, t0, c0, c1):
-            engine_copy(
-                y_mx[0][:, c0:c1, t0 : t0 + 2].rearrange("p (c i) t -> p c i t", i=4),
-                res[:, t0 : t0 + 2, c0:c1].rearrange("p t (c i) -> p c i t", i=4),
-            )
-
-        cv[0] = keep.tile([P, W], F32, name="cv0")
-        sig[0] = keep.tile([P, W], F32, name="sig0")
-        lo = psum.tile([P, W], F32, name="a_ps")
-        hi = psum.tile([P, W], F32, name="u_ps")
-        product(lo, z_mx[1], z_mx[2], 0, z2_mx, 0, 256)
-        product(hi, z_mx[1], z_mx[2], 0, z2_mx, 256, 512)
-        for dst in (wins[0], cv[0]):
-            nc.scalar.activation(dst[:, 0:256], lo[:, 0:256], ACT.Copy, scale=0.0625)
-            nc.vector.tensor_scalar_mul(dst[:, 256:512], hi[:, 256:512], 0.0625)
-        moments(1)
+        low, high = bank("a_ps"), bank("sum_ps")
+        product(low, z_mx, 0, z2_mx, HALVES[0])
+        product(high, z_mx, 0, z2_mx, HALVES[1])
+        for dst in (windows[0], cv[0]):
+            nc.scalar.activation(dst[:, HALVES[0]], low[:, HALVES[0]], ACT.Copy, scale=CV_SCALE)
+            nc.vector.tensor_scalar_mul(dst[:, HALVES[1]], high[:, HALVES[1]], CV_SCALE)
+        make_cv(1, "b_ps")
         fetch(0)
-        moments(2)
+        make_cv(2, "a_ps")
         fetch(1)
         send(0)
         squash(0)
-        moments(3)
+        make_cv(LAST, "b_ps")
         fetch(2)
         send(1)
         squash(1)
         squash(2)
-        fetch(3)
-        squash(3)
-        gate(0, 0, W)
+        fetch(LAST)
+        squash(LAST)
+        gate(0, WHOLE)
         send(2)
-        gate(1, 0, W)
-        pair(nc.scalar.copy, 0, 0, W)
-        gate(2, 0, W)
-        send(3)
-        gate(3, 256, 512)
-        gate(3, 0, 256)
-        pair(nc.scalar.copy, 2, 384, 512)
-        pair(nc.vector.tensor_copy, 2, 256, 384)
-        pair(nc.vector.tensor_copy, 2, 0, 256)
+        gate(1, WHOLE)
+        group_out(nc.scalar.copy, 0, WHOLE)
+        gate(2, WHOLE)
+        send(LAST)
+        gate(LAST, HALVES[1])
+        gate(LAST, HALVES[0])
+        group_out(nc.scalar.copy, 2, BLOCKS[3])
+        group_out(nc.vector.tensor_copy, 2, BLOCKS[2])
+        group_out(nc.vector.tensor_copy, 2, HALVES[0])
+
         words_out = out_1[0].rearrange("p n t -> p (n t)").bitcast(I32)
-        for c0 in (256, 0):
-            quantise(y_mx, c0, c0 + 256)
-            nc.sync.dma_start(words_out[:, c0 : c0 + 256], y_mx[1][:, c0 : c0 + 256])
+        for cols in reversed(HALVES):
+            quantise(out_mx, cols)
+            nc.sync.dma_start(words_out[:, cols], out_mx[1][:, cols])
         for q in range(4):
-            eng = nc.sync if q % 2 == 0 else nc.scalar
-            eng.dma_start(out_2[0, 4 * q : 4 * q + 4, :].bitcast(I32), y_mx[2][32 * q : 32 * q + 4, :].bitcast(I32))
+            queue = nc.sync if q % 2 == 0 else nc.scalar
+            queue.dma_start(
+                out_2[0, 4 * q : 4 * q + 4, :].bitcast(I32), out_mx[2][32 * q : 32 * q + 4, :].bitcast(I32)
+            )

@@ -158,7 +158,7 @@ def tile_picked_momtop2sendg_none_po_kernel(
             )
             return words
 
-        wa_mx, wb_mx, z_mx, z2_mx, out_mx = (mx_operand(name) for name in ("wa", "wb", "z", "z2", "out"))
+        wa_mx, wb_mx, z_mx, z2_mx = (mx_operand(name) for name in ("wa", "wb", "z", "z2"))
 
         xa_picked = pick_scales(offs_t, "xa_picked")
         xb_picked = pick_scales(two_t, "xb_picked")
@@ -180,7 +180,7 @@ def tile_picked_momtop2sendg_none_po_kernel(
         a_last = bank("b_ps")
         product(a_last, xa_mx, LAST, wa_mx, WHOLE)
 
-        gates = bank("b_ps")
+        gates = bank("a_ps")
         nc.tensor.transpose(gates[:, 0:P], gate_rows[:], ident[:])
         half_size = keep.tile([P, PACK], F32, name="half_size")
         sign = keep.tile([P, PACK], F32, name="sign")
@@ -308,33 +308,49 @@ def tile_picked_momtop2sendg_none_po_kernel(
         sent = [keep.tile([P, WINDOW], F32, name=f"sent{u}") for u in range(PACK)]
         squashed = [plane(f"squashed{u}") for u in range(PACK)]
         gap = [plane(f"gap{u}") for u in range(PACK)]
-        rise = [plane(f"rise{u}") for u in range(PACK)]
+        rise = [plane(f"rise{u}") for u in range(LAST)]
+        rise.append(keep.tile([P, W], F32, name="rise3", tag="out_values", align_bytes=64))
+        out_mx = mx_operand("out")
 
         def group_out(engine_copy, u, cols):
             engine_copy(
                 out_mx[0][:, cols, u : u + 2].rearrange("p (c i) j -> p c i j", i=4),
                 result[:, u : u + 2, cols].rearrange("p j (c i) -> p c i j", i=4),
             )
-        cv = [plane(f"cv{u}") for u in range(PACK)]
+        cv = [plane("cv0"), plane("cv1")]
+        cv_turned = {u: plane(f"cv_turned{u}") for u in (2, LAST)}
+        larger = {u: plane(f"larger{u}") for u in (2, LAST)}
 
-        def make_cv(u, tag):
+        def make_cv(u, tag, copies):
             acc = bank(tag)
             product(acc, z_mx, u, z2_mx, WHOLE)
-            for dst in (windows[u], cv[u]):
+            for dst in copies:
                 nc.scalar.activation(dst[:, WHOLE], acc[:], ACT.Copy, scale=CV_SCALE)
 
         def fetch(u):
             nc.vector.tensor_tensor(gap[u][:], windows[u][:].indirect(n5_t[:]), cv[u][:], ALU.subtract)
-            nc.scalar.activation(rise[u][:], gap[u][:], ACT.Relu)
 
-        def send(u):
+        def send_sum(u):
+            nc.scalar.activation(rise[u][:], gap[u][:], ACT.Relu)
             nc.vector.tensor_tensor(sent[u][:].indirect(n4_t[:]), rise[u][:], cv[u][:], ALU.add)
 
+        def fetch_negated(u):
+            nc.vector.tensor_scalar(gap[u][:], windows[u][:].indirect(n5_t[:]), -1.0, 0.0, ALU.mult, ALU.add)
+
+        def make_larger(u):
+            nc.scalar.copy(cv_turned[u][:], add_turned("b_ps", [windows[u]])[:])
+            nc.scalar.activation(rise[u][:], add_turned("sum_ps", [windows[u], gap[u]])[:], ACT.Relu, scale=-1.0)
+            nc.scalar.copy(larger[u][:], add_turned("back_ps", [cv_turned[u], rise[u]])[:])
+
+        def send(u):
+            nc.vector.tensor_copy(sent[u][:].indirect(n4_t[:]), larger[u][:])
+
         def squash(u):
-            nc.scalar.activation(squashed[u][:], cv[u][:], ACT.Sigmoid)
+            nc.scalar.activation(squashed[u][:], windows[u][:, WHOLE], ACT.Sigmoid)
 
         def gate(u, cols):
-            nc.vector.tensor_tensor(result[:, u, cols], sent[u][:, cols], squashed[u][:, cols], ALU.mult)
+            engine = nc.vector if u == LAST else nc.gpsimd
+            engine.tensor_tensor(result[:, u, cols], sent[u][:, cols], squashed[u][:, cols], ALU.mult)
             nc.sync.dma_start(out_rows[:, u, cols], result[:, u, cols])
 
         low, high = bank("a_ps"), bank("sum_ps")
@@ -343,24 +359,26 @@ def tile_picked_momtop2sendg_none_po_kernel(
         for dst in (windows[0], cv[0]):
             nc.scalar.activation(dst[:, HALVES[0]], low[:, HALVES[0]], ACT.Copy, scale=CV_SCALE)
             nc.vector.tensor_scalar_mul(dst[:, HALVES[1]], high[:, HALVES[1]], CV_SCALE)
-        make_cv(1, "b_ps")
+        make_cv(1, "b_ps", (windows[1], cv[1]))
         fetch(0)
-        make_cv(2, "a_ps")
+        make_cv(2, "a_ps", (windows[2],))
         fetch(1)
-        send(0)
+        make_cv(LAST, "a_ps", (windows[LAST],))
+        fetch_negated(2)
+        fetch_negated(LAST)
+        send_sum(0)
+        send_sum(1)
+        make_larger(2)
         squash(0)
-        make_cv(LAST, "b_ps")
-        fetch(2)
-        send(1)
         squash(1)
-        squash(2)
-        fetch(LAST)
-        squash(LAST)
         gate(0, WHOLE)
-        send(2)
         gate(1, WHOLE)
-        group_out(nc.scalar.copy, 0, WHOLE)
+        send(2)
+        make_larger(LAST)
+        squash(2)
+        squash(LAST)
         gate(2, WHOLE)
+        group_out(nc.scalar.copy, 0, WHOLE)
         send(LAST)
         gate(LAST, HALVES[1])
         gate(LAST, HALVES[0])

@@ -87,8 +87,6 @@ def tile_picked_momtop2sendg_none_po_kernel(
 
         ident = keep.tile([P, P], F32, name="ident")
         make_identity(nc, ident[:])
-        warm = keep.tile([P, 1], F32, name="warm")
-        nc.scalar.activation(warm[:], ident[:, 0:1], ACT.Sigmoid)
 
         windows = []
         for t in range(PACK):
@@ -98,7 +96,7 @@ def tile_picked_momtop2sendg_none_po_kernel(
 
         def mx_operand(name):
             values = keep.tile([P, W, PACK], BF16, name=f"{name}_values", tag=f"{name}_values", align_bytes=64)
-            words = keep.tile([P, W], I32, name=f"{name}_words", align_bytes=64)
+            words = keep.tile([P, W], I32, name=f"{name}_words", tag=f"{name}_words", align_bytes=64)
             scales = keep.tile([P, W], U8, name=f"{name}_scales", align_bytes=64)
             return values, words, scales
 
@@ -158,7 +156,7 @@ def tile_picked_momtop2sendg_none_po_kernel(
             )
             return words
 
-        wa_mx, wb_mx, z_mx, z2_mx = (mx_operand(name) for name in ("wa", "wb", "z", "z2"))
+        wa_mx, wb_mx, z_mx = (mx_operand(name) for name in ("wa", "wb", "z"))
 
         xa_picked = pick_scales(offs_t, "xa_picked")
         xb_picked = pick_scales(two_t, "xb_picked")
@@ -197,7 +195,9 @@ def tile_picked_momtop2sendg_none_po_kernel(
         b1 = [plane("b1_0"), plane("b1_1"), x01[0], size[2]]
         x = [x01[0], x01[1], x01[1], size[1]]
         top = [plane(f"top{t}") for t in range(PACK)]
-        k = [plane(f"k{t}") for t in range(PACK)]
+        cut = [plane(f"cut{t}") for t in range(LAST)]
+        cut.append(keep.tile([P, W], F32, name="cut3", tag="z2_words", align_bytes=64))
+        z2_mx = mx_operand("z2")
         rest = [plane(f"rest{t}") for t in range(PACK)]
         e = {t: plane(f"e{t}") for t in (2, LAST)}
         turned = {}
@@ -221,22 +221,22 @@ def tile_picked_momtop2sendg_none_po_kernel(
                 e[t][:, cols], windows[t][:].indirect(n3_t[:, entries(cols)]), top[t][:, cols], ALU.subtract
             )
 
-        def make_k(t, cols):
-            nc.vector.scalar_tensor_tensor(k[t][:, cols], e[t][:, cols], -1.0, size[t][:, cols], ALU.mult, ALU.min)
+        def make_cut(t, cols):
+            nc.vector.scalar_tensor_tensor(cut[t][:, cols], e[t][:, cols], -1.0, size[t][:, cols], ALU.mult, ALU.min)
 
         def make_excess(t):
             nc.scalar.activation(rest[t][:], e[t][:, WHOLE], ACT.Relu, scale=3.0)
 
         def add_up(t):
             turned[t] = ring.tile([P, W], F32, name="turned")
-            nc.scalar.copy(turned[t][:], add_turned("sum_ps", [top[t], rest[t], k[t]])[:])
+            nc.scalar.copy(turned[t][:], add_turned("sum_ps", [top[t], rest[t], cut[t]])[:])
 
         def turn_back(t):
             acc = add_turned("back_ps", [turned[t]])
             nc.scalar.activation(z_planes[:, t, :], acc[:], ACT.Copy, scale=half_size[:, t : t + 1])
 
-        def fold_k(t, cols):
-            nc.vector.scalar_tensor_tensor(rest[t][:, cols], k[t][:, cols], -2.0, k[t][:, cols], ALU.mult, ALU.max)
+        def fold_cut(t, cols):
+            nc.vector.scalar_tensor_tensor(rest[t][:, cols], cut[t][:, cols], -2.0, cut[t][:, cols], ALU.mult, ALU.max)
 
         def add_top(t, cols):
             nc.vector.tensor_tensor(z_planes[:, t, cols], rest[t][:, cols], top[t][:, cols], ALU.add)
@@ -271,12 +271,12 @@ def tile_picked_momtop2sendg_none_po_kernel(
         make_excess(1)
         interleave(z2_mx, z2_planes[:, :, HALVES[0]], HALVES[0])
         fetch_b1(2, WHOLE)
-        make_k(0, WHOLE)
+        make_cut(0, WHOLE)
         fetch_x(2, WHOLE)
         make_size(2)
         add_up(0)
-        make_k(1, WHOLE)
-        in_halves(2, (make_top, fetch_e, make_k))
+        make_cut(1, WHOLE)
+        in_halves(2, (make_top, fetch_e, make_cut))
         interleave(z2_mx, z2_planes[:, :, HALVES[1]], HALVES[1])
         make_excess(2)
         turn_back(0)
@@ -286,22 +286,24 @@ def tile_picked_momtop2sendg_none_po_kernel(
         make_size(LAST)
         turn_back(1)
         turn_back(2)
-        quantise(z2_mx, WHOLE)
-        in_halves(LAST, (make_top, fetch_e, make_k, fold_k, add_top))
+        in_halves(LAST, (make_top, fetch_e, make_cut, fold_cut, add_top))
 
         z_dealt = z_planes[:].rearrange("p t (m u) -> p u m t", u=PACK)
 
         def group_z(engine_copy, u, first, last):
             engine_copy(z_mx[0][:, P * u + first : P * u + last, :], z_dealt[:, u, first:last])
 
-        group_z(nc.vector.tensor_copy, 0, 0, P // 2)
-        group_z(nc.vector.tensor_copy, 0, P // 2, P)
+        group_z(nc.vector.tensor_copy, 2, 0, P // 2)
+        group_z(nc.vector.tensor_copy, 2, P // 2, P)
+        group_z(nc.scalar.copy, 0, 0, P)
         group_z(nc.scalar.copy, 1, 0, P)
-        group_z(nc.scalar.copy, 2, 0, P)
+        quantise(z2_mx, HALVES[0])
+        quantise(z_mx, BLOCKS[2])
+        quantise(z2_mx, HALVES[1])
         quantise(z_mx, BLOCKS[0])
-        group_z(nc.vector.tensor_copy, 3, 0, P)
+        group_z(nc.vector.tensor_copy, LAST, 0, P)
         quantise(z_mx, BLOCKS[1])
-        quantise(z_mx, HALVES[1])
+        quantise(z_mx, BLOCKS[LAST])
 
         out_rows = out_0.rearrange("(p u) c -> p u c", u=PACK)
         result = keep.tile([P, PACK, W], F32, name="result")
@@ -317,6 +319,7 @@ def tile_picked_momtop2sendg_none_po_kernel(
                 out_mx[0][:, cols, u : u + 2].rearrange("p (c i) j -> p c i j", i=4),
                 result[:, u : u + 2, cols].rearrange("p j (c i) -> p c i j", i=4),
             )
+
         cv = [plane("cv0"), plane("cv1")]
         cv_turned = {u: plane(f"cv_turned{u}") for u in (2, LAST)}
         larger = {u: plane(f"larger{u}") for u in (2, LAST)}
@@ -354,17 +357,16 @@ def tile_picked_momtop2sendg_none_po_kernel(
             nc.sync.dma_start(out_rows[:, u, cols], result[:, u, cols])
 
         low, high = bank("a_ps"), bank("sum_ps")
-        product(low, z_mx, 0, z2_mx, HALVES[0])
-        product(high, z_mx, 0, z2_mx, HALVES[1])
-        for dst in (windows[0], cv[0]):
-            nc.scalar.activation(dst[:, HALVES[0]], low[:, HALVES[0]], ACT.Copy, scale=CV_SCALE)
-            nc.vector.tensor_scalar_mul(dst[:, HALVES[1]], high[:, HALVES[1]], CV_SCALE)
-        make_cv(1, "b_ps", (windows[1], cv[1]))
-        fetch(0)
-        make_cv(2, "a_ps", (windows[2],))
-        fetch(1)
-        make_cv(LAST, "a_ps", (windows[LAST],))
+        product(low, z_mx, 2, z2_mx, HALVES[0])
+        product(high, z_mx, 2, z2_mx, HALVES[1])
+        nc.scalar.activation(windows[2][:, HALVES[0]], low[:, HALVES[0]], ACT.Copy, scale=CV_SCALE)
+        nc.vector.tensor_scalar_mul(windows[2][:, HALVES[1]], high[:, HALVES[1]], CV_SCALE)
+        make_cv(0, "b_ps", (windows[0], cv[0]))
         fetch_negated(2)
+        make_cv(1, "a_ps", (windows[1], cv[1]))
+        fetch(0)
+        make_cv(LAST, "b_ps", (windows[LAST],))
+        fetch(1)
         fetch_negated(LAST)
         send_sum(0)
         send_sum(1)

from contextlib import ExitStack

import concourse.mybir as mybir
from concourse.masks import make_identity

FLOPS = 3 * 2 * 512 * 512 * 512

F32 = mybir.dt.float32
BF16 = mybir.dt.bfloat16
I32 = mybir.dt.int32
U32 = mybir.dt.uint32
U16 = mybir.dt.uint16
U8 = mybir.dt.uint8
FP8X4 = mybir.dt.float8_e4m3fn_x4
ALU = mybir.AluOpType
ACT = mybir.ActivationFunctionType

P = 128
PACK = 4
TOKENS = 2048
W = 512
HALF = W // 2
WINDOW = 2 * W
LAST = PACK - 1
CV_SCALE = 0.0625
WHOLE = slice(0, W)
HALVES = (slice(0, HALF), slice(HALF, W))
BLOCKS = tuple(slice(P * q, P * (q + 1)) for q in range(W // P))


def entries(cols):
    return slice(cols.start // 16, cols.stop // 16)


def tile_picked_momtop2sendg_none_po_kernel(
    tc, x_words, x_scales, wa, wb, gt, gi, offs, two, n1, n2, n3, n4, n5, out_0, out_1, out_2
):
    nc = tc.nc
    with ExitStack() as ctx:
        lists = ctx.enter_context(tc.tile_pool(name="lists", bufs=1))
        keep = ctx.enter_context(tc.tile_pool(name="keep", bufs=1))
        ring = ctx.enter_context(tc.tile_pool(name="ring", bufs=2))
        psum = ctx.enter_context(tc.psum_pool(name="psum", bufs=2))

        def plane(name):
            return keep.tile([P, W], F32, name=name)

        def bank(tag):
            return psum.tile([P, W], F32, name=tag)

        def load_list(src, name):
            tile = lists.tile([P, W // 16], U16, name=name)
            nc.sync.dma_start(tile[:], src)
            return tile

        def load_weight(w, name, cols):
            raw = keep.tile([P, PACK, cols.stop - cols.start], F32, name=name)
            nc.sync.dma_start(raw[:], w.rearrange("(p j) c -> p j c", j=PACK)[:, :, cols])
            return raw

        x_scale_rows = keep.tile([P, TOKENS], U8, name="x_scale_rows")
        nc.gpsimd.memset(x_scale_rows[:].bitcast(I32), 0)
        gate_rows = keep.tile([P, P], F32, name="gate_rows")
        nc.gpsimd.memset(gate_rows[:], 0.0)

        offs_t = load_list(offs, "offs_t")
        two_t = load_list(two, "two_t")
        wa_raw = [load_weight(wa, "wa_raw0", HALVES[0])]
        for q in range(4):
            nc.sync.dma_start(
                x_scale_rows[32 * q : 32 * q + 4, :].bitcast(I32), x_scales[0, 4 * q : 4 * q + 4, :].bitcast(I32)
            )
        wa_raw.append(load_weight(wa, "wa_raw1", HALVES[1]))
        x_word_rows = keep.tile([P, TOKENS], I32, name="x_word_rows")
        nc.sync.dma_start(x_word_rows[:], x_words[0].rearrange("p n t -> p (n t)").bitcast(I32))
        n1_t = load_list(n1, "n1_t")
        n2_t = load_list(n2, "n2_t")
        n3_t = load_list(n3, "n3_t")
        for first_row, gate_in in ((0, gt), (PACK, gi)):
            nc.sync.dma_start(
                gate_rows[first_row : first_row + PACK, :].rearrange("t (b r) -> t b r", r=8),
                gate_in.rearrange("(b t r) o -> t b (r o)", t=PACK, r=8),
            )
        wb_raw = load_weight(wb, "wb_raw", WHOLE)
        n5_t = load_list(n5, "n5_t")
        n4_t = load_list(n4, "n4_t")

        ident = keep.tile([P, P], F32, name="ident")
        make_identity(nc, ident[:])

        windows = []
        for t in range(PACK):
            window = keep.tile([P, WINDOW], F32, name=f"window{t}")
            nc.gpsimd.memset(window[:, W:], 0.0)
            windows.append(window)

        def mx_operand(name):
            values = keep.tile([P, W, PACK], BF16, name=f"{name}_values", tag=f"{name}_values", align_bytes=64)
            words = keep.tile([P, W], I32, name=f"{name}_words", tag=f"{name}_words", align_bytes=64)
            scales = keep.tile([P, W], U8, name=f"{name}_scales", align_bytes=64)
            return values, words, scales

        def interleave(mx, src, cols):
            nc.scalar.copy(
                mx[0][:, cols, :].rearrange("p (c i) j -> p c j i", i=4),
                src.rearrange("p j (c i) -> p c j i", i=4),
            )

        def quantise(mx, cols):
            values, words, scales = mx
            nc.vector.quantize_mx(
                out=words[:, cols].bitcast(FP8X4),
                scales=scales[:, cols],
                in_=values[:, cols, :].rearrange("p c j -> p (c j)"),
            )

        def product(acc, left, t, right, cols):
            nc.tensor.matmul_mx(
                out=acc[:, cols],
                lhsT=left[1][:, BLOCKS[t]].bitcast(FP8X4),
                lhsT_scale=left[2][:, BLOCKS[t]],
                rhs=right[1][:, cols].bitcast(FP8X4),
                rhs_scale=right[2][:, cols],
                start=True,
                stop=True,
            )

        def add_turned(tag, terms):
            acc = bank(tag)
            for cols in BLOCKS:
                for i, term in enumerate(terms):
                    nc.tensor.matmul(
                        acc[:, cols], term[:, cols], ident[:],
                        start=(i == 0), stop=(i == len(terms) - 1), is_transpose=True,
                    )
            return acc

        def pick_scales(offsets, name):
            picked = keep.tile([P, W], U8, name=name, align_bytes=64)
            nc.vector.tensor_copy(picked[:], x_scale_rows[:].indirect(offsets[:]))
            return picked

        def deal_scales(picked, name):
            dealt = keep.tile([P, W], U8, name=name, align_bytes=64)
            nc.vector.tensor_copy(
                dealt[:].bitcast(I32).rearrange("p (t b r) -> p b t r", t=PACK, r=2),
                picked[:].bitcast(I32).rearrange("p (b t r) -> p b t r", t=PACK, r=2),
            )
            return dealt

        def pick_words(offsets, name):
            words = keep.tile([P, W], I32, name=name, align_bytes=64)
            nc.vector.tensor_copy(
                words[:].bitcast(U32).rearrange("p (t b r) -> p b t r", t=PACK, r=8),
                x_word_rows[:].bitcast(U32).indirect(offsets[:]),
            )
            return words

        wa_mx, wb_mx, z_mx = (mx_operand(name) for name in ("wa", "wb", "z"))

        xa_picked = pick_scales(offs_t, "xa_picked")
        xb_picked = pick_scales(two_t, "xb_picked")
        xa_scales = deal_scales(xa_picked, "xa_scales")
        xb_scales = deal_scales(xb_picked, "xb_scales")
        for raw, cols in zip(wa_raw, HALVES):
            interleave(wa_mx, raw[:], cols)
            quantise(wa_mx, cols)
        xa_mx = (None, pick_words(offs_t, "xa_words"), xa_scales)

        for cols, tag in zip(HALVES, ("sum_ps", "back_ps")):
            acc = bank(tag)
            product(acc, xa_mx, 0, wa_mx, cols)
            nc.scalar.copy(windows[0][:, cols], acc[:, cols])
        for t in range(1, LAST):
            acc = bank("a_ps")
            product(acc, xa_mx, t, wa_mx, WHOLE)
            nc.scalar.copy(windows[t][:, WHOLE], acc[:])
        a_last = bank("b_ps")
        product(a_last, xa_mx, LAST, wa_mx, WHOLE)

        gates = bank("a_ps")
        nc.tensor.transpose(gates[:, 0:P], gate_rows[:], ident[:])
        half_size = keep.tile([P, PACK], F32, name="half_size")
        sign = keep.tile([P, PACK], F32, name="sign")
        signed_gi = keep.tile([P, PACK], F32, name="signed_gi")
        nc.scalar.activation(half_size[:], gates[:, 0:PACK], ACT.Abs, scale=0.5)
        nc.scalar.activation(sign[:], gates[:, 0:PACK], ACT.Sign)
        nc.scalar.activation(windows[LAST][:, WHOLE], a_last[:], ACT.Copy, scale=half_size[:, LAST : LAST + 1])
        xb_mx = (None, pick_words(two_t, "xb_words"), xb_scales)

        z_planes = keep.tile([P, PACK, W], BF16, name="z_planes")
        z2_planes = keep.tile([P, PACK, W], BF16, name="z2_planes")
        size = [wb_raw[:, t, :] for t in range(PACK)]
        x01 = [plane("x0"), plane("x1")]
        b1 = [plane("b1_0"), plane("b1_1"), x01[0], size[2]]
        x = [x01[0], x01[1], x01[1], size[1]]
        top = [plane(f"top{t}") for t in range(PACK)]
        cut = [plane(f"cut{t}") for t in range(LAST)]
        cut.append(keep.tile([P, W], F32, name="cut3", tag="z2_words", align_bytes=64))
        z2_mx = mx_operand("z2")
        rest = [plane(f"rest{t}") for t in range(PACK)]
        e = {t: plane(f"e{t}") for t in (2, LAST)}
        turned = {}

        def fetch_b1(t, cols):
            nc.vector.tensor_copy(b1[t][:, cols], windows[t][:].indirect(n1_t[:, entries(cols)]))

        def fetch_x(t, cols):
            nc.vector.tensor_tensor(
                x[t][:, cols], windows[t][:].indirect(n2_t[:, entries(cols)]), b1[t][:, cols], ALU.subtract
            )

        def make_size(t):
            nc.scalar.activation(size[t][:, WHOLE], x[t][:, WHOLE], ACT.Abs)

        def make_top(t, cols):
            nc.vector.scalar_tensor_tensor(top[t][:, cols], x[t][:, cols], 0.0, b1[t][:, cols], ALU.max, ALU.add)

        def fetch_e(t, cols):
            nc.vector.tensor_tensor(
                e[t][:, cols], windows[t][:].indirect(n3_t[:, entries(cols)]), top[t][:, cols], ALU.subtract
            )

        def make_cut(t, cols):
            nc.vector.scalar_tensor_tensor(cut[t][:, cols], e[t][:, cols], -1.0, size[t][:, cols], ALU.mult, ALU.min)

        def make_excess(t):
            nc.scalar.activation(rest[t][:], e[t][:, WHOLE], ACT.Relu, scale=3.0)

        def add_up(t):
            turned[t] = ring.tile([P, W], F32, name="turned")
            nc.scalar.copy(turned[t][:], add_turned("sum_ps", [top[t], rest[t], cut[t]])[:])

        def turn_back(t):
            acc = add_turned("back_ps", [turned[t]])
            nc.scalar.activation(z_planes[:, t, :], acc[:], ACT.Copy, scale=half_size[:, t : t + 1])

        def fold_cut(t, cols):
            nc.vector.scalar_tensor_tensor(rest[t][:, cols], cut[t][:, cols], -2.0, cut[t][:, cols], ALU.mult, ALU.max)

        def add_top(t, cols):
            nc.vector.tensor_tensor(z_planes[:, t, cols], rest[t][:, cols], top[t][:, cols], ALU.add)

        def in_halves(t, steps):
            for step in steps:
                for cols in HALVES:
                    step(t, cols)

        for cols in HALVES:
            interleave(wb_mx, wb_raw[:, :, cols], cols)
        in_halves(0, (fetch_b1,))
        fetch_x(0, HALVES[0])
        fetch_b1(1, WHOLE)
        fetch_x(0, HALVES[1])
        fetch_x(1, WHOLE)
        make_size(0)
        make_size(1)
        make_top(0, WHOLE)
        quantise(wb_mx, WHOLE)
        nc.vector.tensor_tensor(signed_gi[:], gates[:, PACK : 2 * PACK], sign[:], ALU.mult)
        for t, tag in enumerate(("b_ps", "b_ps", "back_ps", "back_ps")):
            acc = bank(tag)
            product(acc, xb_mx, t, wb_mx, WHOLE)
            nc.scalar.activation(z2_planes[:, t, :], acc[:], ACT.Copy, scale=signed_gi[:, t : t + 1])
        e01 = keep.tile([P, 2, W], F32, name="e01", tag="wb_values", align_bytes=64)
        e.update({t: e01[:, t, :] for t in (0, 1)})
        make_top(1, WHOLE)
        fetch_e(0, WHOLE)
        fetch_e(1, WHOLE)
        make_excess(0)
        make_excess(1)
        interleave(z2_mx, z2_planes[:, :, HALVES[0]], HALVES[0])
        fetch_b1(2, WHOLE)
        make_cut(0, WHOLE)
        fetch_x(2, WHOLE)
        make_size(2)
        add_up(0)
        make_cut(1, WHOLE)
        in_halves(2, (make_top, fetch_e, make_cut))
        interleave(z2_mx, z2_planes[:, :, HALVES[1]], HALVES[1])
        make_excess(2)
        turn_back(0)
        add_up(1)
        in_halves(LAST, (fetch_b1, fetch_x))
        add_up(2)
        make_size(LAST)
        turn_back(1)
        turn_back(2)
        in_halves(LAST, (make_top, fetch_e, make_cut, fold_cut, add_top))

        z_dealt = z_planes[:].rearrange("p t (m u) -> p u m t", u=PACK)

        def group_z(engine_copy, u, first, last):
            engine_copy(z_mx[0][:, P * u + first : P * u + last, :], z_dealt[:, u, first:last])

        group_z(nc.vector.tensor_copy, 2, 0, P // 2)
        group_z(nc.vector.tensor_copy, 2, P // 2, P)
        group_z(nc.scalar.copy, 0, 0, P)
        group_z(nc.scalar.copy, 1, 0, P)
        quantise(z2_mx, HALVES[0])
        quantise(z_mx, BLOCKS[2])
        quantise(z2_mx, HALVES[1])
        quantise(z_mx, BLOCKS[0])
        group_z(nc.vector.tensor_copy, LAST, 0, P)
        quantise(z_mx, BLOCKS[1])
        quantise(z_mx, BLOCKS[LAST])

        out_rows = out_0.rearrange("(p u) c -> p u c", u=PACK)
        result = keep.tile([P, PACK, W], F32, name="result")
        sent = [keep.tile([P, WINDOW], F32, name=f"sent{u}") for u in range(PACK)]
        squashed = [plane(f"squashed{u}") for u in range(PACK)]
        gap = [plane(f"gap{u}") for u in range(PACK)]
        rise = [plane(f"rise{u}") for u in range(LAST)]
        rise.append(keep.tile([P, W], F32, name="rise3", tag="out_values", align_bytes=64))
        out_mx = mx_operand("out")

        def group_out(engine_copy, u, cols):
            engine_copy(
                out_mx[0][:, cols, u : u + 2].rearrange("p (c i) j -> p c i j", i=4),
                result[:, u : u + 2, cols].rearrange("p j (c i) -> p c i j", i=4),
            )

        cv = [plane("cv0"), plane("cv1")]
        cv_turned = {u: plane(f"cv_turned{u}") for u in (2, LAST)}
        larger = {u: plane(f"larger{u}") for u in (2, LAST)}

        def make_cv(u, tag, copies):
            acc = bank(tag)
            product(acc, z_mx, u, z2_mx, WHOLE)
            for dst in copies:
                nc.scalar.activation(dst[:, WHOLE], acc[:], ACT.Copy, scale=CV_SCALE)

        def fetch(u):
            nc.vector.tensor_tensor(gap[u][:], windows[u][:].indirect(n5_t[:]), cv[u][:], ALU.subtract)

        def send_sum(u):
            nc.scalar.activation(rise[u][:], gap[u][:], ACT.Relu)
            nc.vector.tensor_tensor(sent[u][:].indirect(n4_t[:]), rise[u][:], cv[u][:], ALU.add)

        def fetch_negated(u):
            nc.vector.tensor_scalar(gap[u][:], windows[u][:].indirect(n5_t[:]), -1.0, 0.0, ALU.mult, ALU.add)

        def make_larger(u):
            nc.scalar.copy(cv_turned[u][:], add_turned("b_ps", [windows[u]])[:])
            nc.scalar.activation(rise[u][:], add_turned("sum_ps", [windows[u], gap[u]])[:], ACT.Relu, scale=-1.0)
            nc.scalar.copy(larger[u][:], add_turned("back_ps", [cv_turned[u], rise[u]])[:])

        def send(u):
            nc.vector.tensor_copy(sent[u][:].indirect(n4_t[:]), larger[u][:])

        def squash(u):
            nc.scalar.activation(squashed[u][:], windows[u][:, WHOLE], ACT.Sigmoid)

        def gate(u, cols):
            engine = nc.vector if u == LAST else nc.gpsimd
            engine.tensor_tensor(result[:, u, cols], sent[u][:, cols], squashed[u][:, cols], ALU.mult)
            nc.sync.dma_start(out_rows[:, u, cols], result[:, u, cols])

        low, high = bank("a_ps"), bank("sum_ps")
        product(low, z_mx, 2, z2_mx, HALVES[0])
        product(high, z_mx, 2, z2_mx, HALVES[1])
        nc.scalar.activation(windows[2][:, HALVES[0]], low[:, HALVES[0]], ACT.Copy, scale=CV_SCALE)
        nc.vector.tensor_scalar_mul(windows[2][:, HALVES[1]], high[:, HALVES[1]], CV_SCALE)
        make_cv(0, "b_ps", (windows[0], cv[0]))
        fetch_negated(2)
        make_cv(1, "a_ps", (windows[1], cv[1]))
        fetch(0)
        make_cv(LAST, "b_ps", (windows[LAST],))
        fetch(1)
        fetch_negated(LAST)
        send_sum(0)
        send_sum(1)
        make_larger(2)
        squash(0)
        squash(1)
        gate(0, WHOLE)
        gate(1, WHOLE)
        send(2)
        make_larger(LAST)
        squash(2)
        squash(LAST)
        gate(2, WHOLE)
        group_out(nc.scalar.copy, 0, WHOLE)
        send(LAST)
        gate(LAST, HALVES[1])
        gate(LAST, HALVES[0])
        group_out(nc.scalar.copy, 2, BLOCKS[3])
        group_out(nc.vector.tensor_copy, 2, BLOCKS[2])
        group_out(nc.vector.tensor_copy, 2, HALVES[0])

        words_out = out_1[0].rearrange("p n t -> p (n t)").bitcast(I32)
        for cols in reversed(HALVES):
            quantise(out_mx, cols)
            nc.sync.dma_start(words_out[:, cols], out_mx[1][:, cols])
        for q in range(4):
            queue = nc.sync if q % 2 == 0 else nc.scalar
            queue.dma_start(
                out_2[0, 4 * q : 4 * q + 4, :].bitcast(I32), out_mx[2][32 * q : 32 * q + 4, :].bitcast(I32)
            )
